import numpy as np
import ml_dtypes


def mxq(x, axis, fmt="e4m3"):
    dtype, down = {"e4m3": (ml_dtypes.float8_e4m3fn, 7), "e5m2": (ml_dtypes.float8_e5m2, 14)}[fmt]
    v = np.moveaxis(np.asarray(x, np.float32).astype(ml_dtypes.bfloat16).astype(np.float64), axis, -1)
    blocks = v.reshape(v.shape[:-1] + (-1, 32))
    amax = np.abs(blocks).max(-1, keepdims=True)
    byte = np.maximum(np.where(amax > 0, np.frexp(amax)[1] - 1 + 127, 0) - down, 1)
    scale = np.exp2(byte - 127.0)
    codes = (blocks / scale).astype(np.float32).astype(dtype).astype(np.float64)
    return np.moveaxis((codes * scale).reshape(v.shape), -1, axis)


WIDE = False


def mx_kscale(k):
    if not WIDE:
        return np.ones(k)
    levels = np.array([10, -10, 5, -5, 0])
    if k % 512:
        return np.exp2(np.random.permutation(np.resize(levels, k // 32))).repeat(32)
    a = np.empty((k // 512, 16))
    for p in range(k // 512):
        a[p, :8] = np.random.permutation(np.resize(levels, 8))
        for g in range(8):
            far = levels[np.abs(levels - a[p, g]) >= 10]
            a[p, g + 8] = far[np.random.randint(len(far))]
    return np.exp2(a.ravel()).repeat(32)


def f64(x):
    return np.asarray(x).astype(np.float64)


def striped(idx):
    return np.tile(idx.reshape(-1, 16).T, (8, 1)).astype(np.uint16)


def unstriped(offs):
    return offs[:16].T.reshape(-1).astype(np.int64)


E2M1 = np.array([0.0, 0.5, 1.0, 1.5, 2.0, 3.0, 4.0, 6.0, -0.0, -0.5, -1.0, -1.5, -2.0, -3.0, -4.0, -6.0])


def pack_fp4(w):
    k, n = w.shape
    w = f64(np.asarray(w, np.float32).astype(ml_dtypes.bfloat16)).reshape(k // 32, 32, n)
    amax = np.abs(w).max(1)
    mant, ex = np.frexp(amax / 6.0)
    byte = np.clip(np.where(amax > 0, np.where(mant > 0.5, ex, ex - 1) + 127, 1), 1, 254)
    scaled = (w * np.exp2(127.0 - byte)[:, None, :]).reshape(k, n).astype(np.float32)
    c = np.ascontiguousarray(scaled.reshape(k // 512, 128, 4, n).transpose(0, 1, 3, 2)).astype(ml_dtypes.float4_e2m1fn).view(np.uint8) & 0xF
    words = (c[..., 0::2] | (c[..., 1::2] << 4)).reshape(k // 512, 128, 2 * n)
    return np.ascontiguousarray(words), np.ascontiguousarray(byte.astype(np.uint8).reshape(k // 512, 16, n))


def unpack_fp4(words, scales):
    g, _, n = scales.shape
    words = np.ascontiguousarray(words).reshape(g, 128, n, 2)
    nib = np.empty((g, 128, n, 4), np.uint8)
    nib[..., 0::2] = words & 0xF
    nib[..., 1::2] = words >> 4
    vals = E2M1[nib] * np.repeat(np.exp2(scales.astype(np.float64) - 127.0), 8, axis=1)[..., None]
    return vals.transpose(0, 1, 3, 2).reshape(g * 512, n)


def silu(v):
    return v / (1.0 + np.exp(-np.maximum(v, -700.0)))

def planes(y):
    n, m = y.shape
    v = y.astype(np.float32).astype(ml_dtypes.bfloat16).astype(np.float64).reshape(n // 32, 32, m)
    top = np.abs(v).max(1)
    byte = np.clip(np.where(top > 0, np.frexp(top)[1] - 1 + 127 - 7, 1), 1, 254)
    codes = (v * np.exp2(127.0 - byte)[:, None, :]).reshape(n, m).astype(np.float32).astype(ml_dtypes.float8_e4m3fn).view(np.uint8)
    words = codes.reshape(n // 512, 128, 4, m).transpose(0, 1, 3, 2)
    return np.ascontiguousarray(words), np.ascontiguousarray(byte.astype(np.uint8).reshape(n // 512, 16, m))


K, T, H = 1024, 512, 512


def setup_inputs():
    n = np.random.standard_normal
    s = mx_kscale(K)[:, None]
    u = mx_kscale(H)
    packed_xT = pack_fp4(n((K, T)) * s)
    return {
        "x_words": packed_xT[0],
        "x_scales": packed_xT[1],
        "w1": (n((K, H)) / np.sqrt(2 * K) / s * u).astype(np.float32),
        "w2": (n((K, H)) / np.sqrt(2 * K) / s * u).astype(np.float32),
        "w3": (n((H, H)) / np.sqrt(H) / u[:, None]).astype(np.float32),
        "pos1": striped(np.random.permutation(T)),
        "pos2": striped(np.random.permutation(T)),
        "pos3": striped(np.random.permutation(T)),
        "pos4": striped(np.random.permutation(T)),
    }


def reference(x_words, x_scales, w1, w2, w3, pos1, pos2, pos3, pos4):
    xq = unpack_fp4(x_words, x_scales)
    y = mxq(f64(w1), 0, "e4m3").T @ xq
    e = mxq(f64(w2), 0, "e4m3").T @ xq
    z = np.maximum(np.maximum(np.maximum(silu(y + e[:, unstriped(pos1)]), silu(y + e[:, unstriped(pos2)])), silu(y + e[:, unstriped(pos3)])), silu(y + e[:, unstriped(pos4)]))
    out_0 = mxq(f64(w3), 0, "e4m3").T @ mxq(z, 0, "e4m3")
    return (out_0,) + planes(out_0)

@@ -1,0 +1,272 @@
+from contextlib import ExitStack
+
+import concourse.mybir as mybir
+
+K, T, H, D = 1024, 512, 512, 4
+P = 128
+PACK = 4
+PASSES = K // (P * PACK)
+VB = T // P
+WINDOW = 704
+
+FLOPS = 2 * K * H * T * 2 + 2 * H * H * T
+
+F32 = mybir.dt.float32
+BF16 = mybir.dt.bfloat16
+I32 = mybir.dt.int32
+U32 = mybir.dt.uint32
+U16 = mybir.dt.uint16
+U8 = mybir.dt.uint8
+FP8X4 = mybir.dt.float8_e4m3fn_x4
+FP4X4 = mybir.dt.float4_e2m1fn_x4
+SILU = mybir.ActivationFunctionType.Silu
+MAX = mybir.AluOpType.max
+ADD = mybir.AluOpType.add
+
+
+def tile_picked_wedgecv_silu_lo_kernel(tc, x_words, x_scales, w1, w2, w3, pos1, pos2, pos3, pos4, out_0, out_1, out_2):
+    nc = tc.nc
+    with ExitStack() as ctx:
+        keep = ctx.enter_context(tc.tile_pool(name="keep", bufs=1))
+        psum = ctx.enter_context(tc.psum_pool(name="psum", bufs=1))
+
+        def sb(name, shape, dtype):
+            return keep.tile(shape, dtype, name=name, align_bytes=64)
+
+        lists = [sb("list%d" % d, [P, T // 16], U16) for d in range(D)]
+        xw = sb("xw", [P, PASSES, 2 * T], U8)
+        xs = sb("xs", [P, PASSES, T], U8)
+        zeros = sb("zeros", [P, WINDOW - T], F32)
+        e_win = [sb("e%d" % t, [P, WINDOW], F32) for t in range(PACK)]
+        y_sb = [sb("y%d" % t, [P, T], F32) for t in range(PACK)]
+
+        nc.gpsimd.memset(xs[:].bitcast(I32), 0)
+        for q in range(4):
+            nc.sync.dma_start(
+                xs[32 * q : 32 * q + 4, :, :].bitcast(I32),
+                x_scales[:, 4 * q : 4 * q + 4, :].rearrange("z r c -> r z c").bitcast(I32),
+            )
+        nc.gpsimd.memset(zeros[:], 0.0)
+        for t in range(PACK):
+            nc.scalar.activation(e_win[t][:, T:], zeros[:], SILU)
+
+        raw = {}
+
+        def load_w(m, w, z):
+            raw[(m, z)] = sb("raw%d_%d" % (m, z), [P, PACK, H], F32)
+            nc.sync.dma_start(raw[(m, z)][:], w[z * 512 : (z + 1) * 512, :].rearrange("(p j) c -> p j c", j=PACK))
+
+        load_w(0, w2, 0)
+        load_w(0, w2, 1)
+        nc.sync.dma_start(xw[:].bitcast(I32), x_words.rearrange("z p b -> p z b").bitcast(I32))
+        nc.sync.dma_start(lists[0][:], pos1)
+        load_w(1, w1, 0)
+        nc.sync.dma_start(lists[1][:], pos2)
+        load_w(1, w1, 1)
+        for tl, src in zip(lists[2:], (pos3, pos4)):
+            nc.sync.dma_start(tl[:], src)
+        load_w(2, w3, 0)
+
+        banks = [psum.tile([P, T], F32, name="bank%d" % i) for i in range(4)]
+        wq = {}
+        stage = {}
+
+        def prep(m, z, h, eng):
+            stage[(m, z, h)] = sb("wb%d_%d_%d" % (m, z, h), [P, T], F32)
+            wb = stage[(m, z, h)][:].bitcast(BF16)
+            codes = sb("wc%d_%d_%d" % (m, z, h), [P, 2 * P], U32)
+            scales = sb("ws%d_%d_%d" % (m, z, h), [P, 2 * P], U8)
+            wq[(m, z, h)] = (codes, scales)
+            dst = wb.rearrange("p (t c j) -> p c j t", t=2, j=PACK)
+            src = raw[(m, z)][:].rearrange("p j (c t) -> p c j t", t=PACK)[:, :, :, 2 * h : 2 * h + 2]
+            if eng == "v":
+                nc.vector.tensor_copy(dst, src)
+            elif eng == "g":
+                nc.gpsimd.tensor_copy(dst, src)
+            else:
+                nc.scalar.copy(dst, src)
+            nc.vector.quantize_mx(codes[:].bitcast(FP8X4), scales[:], wb)
+
+        def project(m, t, b):
+            acc = banks[b]
+            cols = slice((t % 2) * P, (t % 2 + 1) * P)
+            for z in range(PASSES):
+                codes, scales = wq[(m, z, t // 2)]
+                nc.tensor.matmul_mx(
+                    acc[:], lhsT=codes[:, cols].bitcast(FP8X4), lhsT_scale=scales[:, cols],
+                    rhs=xw[:, z, :].bitcast(FP4X4), rhs_scale=xs[:, z, :], start=z == 0, stop=z == PASSES - 1,
+                )
+            nc.scalar.copy(e_win[t][:, :T] if m == 0 else y_sb[t][:], acc[:])
+
+        ua = [sb("ua%d" % d, [P, 2, T], F32) for d in range(D)]
+        ub = {}
+        mid = {}
+
+        def sums(t, d, v0, n):
+            return ua[d][:, t, v0 : v0 + n] if t < 2 else ub[(v0, d)][:, t - 2, :]
+        early = {}
+
+        def window(t, d, v0, n):
+            return e_win[t][:].indirect(lists[d][:, v0 // 16 : (v0 + n) // 16])
+
+        def fetch(t, d, held=None):
+            early[(t, d)] = sb("g%d_%d" % (t, d), [P, T], F32) if held is None else stage[held]
+            nc.vector.tensor_copy(early[(t, d)][:], window(t, d, 0, T))
+
+        def centre(t, d, v0=0, n=T):
+            nc.vector.tensor_tensor(sums(t, d, v0, n), early[(t, d)][:, v0 : v0 + n], y_sb[t][:, v0 : v0 + n], ADD)
+
+        def fused(t, d, v0=0, n=T):
+            nc.vector.tensor_tensor(sums(t, d, v0, n), window(t, d, v0, n), y_sb[t][:, v0 : v0 + n], ADD)
+
+        oc = sb("oc", [P, T], U32)
+        os_ = sb("os", [P, T], U8)
+        out_rows = out_0.rearrange("(p t) v -> p t v", t=PACK)
+        out_words = out_1[0].rearrange("p c r -> p (c r)").bitcast(I32)
+        s = {}
+        zb = {}
+        obs = {}
+
+        best = sb("best", [P, 2, 2 * T], BF16)
+        part = {}
+
+        def act(h, d, v0, n):
+            if (h, v0) not in s:
+                s[(h, v0)] = sb("s%d_%d" % (h, v0), [P, D, n, 2], BF16)
+            nc.scalar.activation(s[(h, v0)][:, d], (ua[d][:, :, v0 : v0 + n] if h == 0 else ub[(v0, d)]).rearrange("p t v -> p v t"), SILU)
+
+        def pool(h, v0, n):
+            m = sb("m%d_%d" % (h, v0), [P, 2, 2 * n], BF16)
+            mid[(h, v0)] = m
+            src = s[(h, v0)][:].rearrange("p d v t -> p d (v t)")
+            nc.vector.tensor_tensor(m[:], src[:, 0:2, :], src[:, 2:4, :], MAX)
+            nc.vector.tensor_tensor(best[:, h, 2 * v0 : 2 * (v0 + n)], m[:, 0, :], m[:, 1, :], MAX)
+
+        def pool_step(h, v0, n, d):
+            src = s[(h, v0)][:].rearrange("p d v t -> p d (v t)")
+            dst = sb("mp%d_%d" % (v0, d), [P, 2 * n], BF16)[:] if d < D - 1 else best[:, h, 2 * v0 : 2 * (v0 + n)]
+            nc.vector.tensor_tensor(dst, src[:, 0, :] if d == 1 else part[v0], src[:, d, :], MAX)
+            part[v0] = dst
+
+        def weave(v0, n, eng="s"):
+            zb[v0] = sb("zb%d" % v0, [P, n * PACK], BF16)
+            dst = zb[v0][:].bitcast(F32).rearrange("p (v h) -> p v h", h=2)
+            src = best[:].bitcast(F32)[:, :, v0 : v0 + n].rearrange("p h v -> p v h")
+            if eng == "s":
+                nc.scalar.copy(dst, src)
+            else:
+                nc.vector.tensor_copy(dst, src)
+
+        def result(v0, n, how):
+            cols = slice(v0, v0 + n)
+            zc = sb("zc%d" % v0, [P, n], U32)
+            zs = sb("zs%d" % v0, [P, n], U8)
+            nc.vector.quantize_mx(zc[:].bitcast(FP8X4), zs[:], zb[v0][:])
+            acc = psum.tile([P, PACK, n], F32, name="res", tag="res", bufs=4)
+            for t in range(PACK):
+                codes, scales = wq[(2, 0, t // 2)]
+                tc_ = slice((t % 2) * P, (t % 2 + 1) * P)
+                nc.tensor.matmul_mx(
+                    acc[:, t, :], lhsT=codes[:, tc_].bitcast(FP8X4), lhsT_scale=scales[:, tc_],
+                    rhs=zc[:].bitcast(FP8X4), rhs_scale=zs[:], start=True, stop=True,
+                )
+            o32 = sb("o32_%d" % v0, [P, PACK, n], F32)
+            ob = sb("ob%d" % v0, [P, n, PACK], BF16)
+            if how == "p":
+                nc.vector.tensor_copy(ob[:], acc[:].rearrange("p t v -> p v t"))
+            elif how == "s":
+                nc.scalar.copy(ob[:], acc[:].rearrange("p t v -> p v t"))
+            nc.scalar.copy(o32[:], acc[:])
+            nc.sync.dma_start(out_rows[:, :, cols], o32[:])
+            obs[v0] = ob
+
+        def planes(v0, n):
+            cols = slice(v0, v0 + n)
+            nc.vector.quantize_mx(oc[:, cols].bitcast(FP8X4), os_[:, cols], obs[v0][:].rearrange("p v t -> p (v t)"))
+            nc.sync.dma_start(out_words[:, cols], oc[:, cols].bitcast(I32))
+
+        def piece(v0, n, ds=range(D), held=None):
+            for d in ds:
+                if held is None:
+                    ub[(v0, d)] = sb("ub%d_%d" % (v0, d), [P, 2, n], F32)[:]
+                else:
+                    ub[(v0, d)] = held.bitcast(F32)[:, : 2 * n].rearrange("p (t v) -> p t v", t=2)
+                for t in (2, 3):
+                    fused(t, d, v0, n)
+                act(1, d, v0, n)
+
+        def last_result(v0, n):
+            cols = slice(v0, v0 + n)
+            zc = sb("zc%d" % v0, [P, n], U32)
+            zs = sb("zs%d" % v0, [P, n], U8)
+            nc.vector.quantize_mx(zc[:].bitcast(FP8X4), zs[:], zb[v0][:])
+            accs = [banks[h][:, : 2 * n].rearrange("p (t v) -> p t v", t=2) for h in range(2)]
+            for t in range(PACK):
+                codes, scales = wq[(2, 0, t // 2)]
+                tc_ = slice((t % 2) * P, (t % 2 + 1) * P)
+                nc.tensor.matmul_mx(
+                    accs[t // 2][:, t % 2, :], lhsT=codes[:, tc_].bitcast(FP8X4), lhsT_scale=scales[:, tc_],
+                    rhs=zc[:].bitcast(FP8X4), rhs_scale=zs[:], start=True, stop=True,
+                )
+            o32 = sb("o32_%d" % v0, [P, PACK, n], F32)
+            ob = sb("ob%d" % v0, [P, n, PACK], BF16)
+            for h in range(2):
+                nc.scalar.copy(o32[:, 2 * h : 2 * h + 2, :], accs[h])
+            nc.sync.dma_start(out_rows[:, :, cols], o32[:])
+            nc.vector.tensor_copy(ob[:].rearrange("p (c i) t -> p c t i", i=4), o32[:].rearrange("p t (c i) -> p c t i", i=4))
+            obs[v0] = ob
+
+        prep(0, 0, 0, "v")
+        prep(0, 0, 1, "v")
+        prep(0, 1, 0, "v")
+        project(0, 0, 0)
+        fetch(0, 0)
+        prep(0, 1, 1, "s")
+        project(0, 1, 1)
+        prep(1, 0, 0, "s")
+        fetch(0, 1)
+        prep(1, 1, 0, "v")
+        fetch(0, 2, (1, 1, 0))
+        fetch(0, 3, (1, 0, 0))
+        project(1, 1, 0)
+        project(1, 0, 1)
+        prep(1, 0, 1, "s")
+        prep(1, 1, 1, "s")
+        project(0, 2, 0)
+        project(0, 3, 1)
+        project(1, 2, 2)
+        project(1, 3, 3)
+        prep(2, 0, 0, "s")
+        for d in range(D):
+            fused(1, d)
+            centre(0, d)
+            act(0, d, 0, T)
+        prep(2, 0, 1, "s")
+        piece(0, P)
+        pool(0, 0, T)
+        pool(1, 0, P)
+        weave(0, P)
+        result(0, P, "s")
+        piece(P, P)
+        planes(0, P)
+        pool(1, P, P)
+        weave(P, P)
+        result(P, P, "s")
+        piece(2 * P, P)
+        planes(P, P)
+        pool(1, 2 * P, P)
+        weave(2 * P, P)
+        result(2 * P, P, "s")
+        piece(3 * P, P, range(2))
+        pool_step(1, 3 * P, P, 1)
+        piece(3 * P, P, range(2, 3))
+        planes(2 * P, P)
+        pool_step(1, 3 * P, P, 2)
+        piece(3 * P, P, range(3, 4))
+        pool_step(1, 3 * P, P, 3)
+        weave(3 * P, P, "v")
+        result(3 * P, P, "p")
+        planes(3 * P, P)
+        for q in range(4):
+            eng = nc.sync if q % 2 == 0 else nc.scalar
+            eng.dma_start(out_2[0, 4 * q : 4 * q + 4, :].bitcast(I32), os_[32 * q : 32 * q + 4, :].bitcast(I32))

@@ -1,6 +1,7 @@
 from contextlib import ExitStack
 
 import concourse.mybir as mybir
+from concourse.masks import make_identity
 
 K, T, H, D = 1024, 512, 512, 4
 P = 128
@@ -8,6 +9,7 @@ PACK = 4
 PASSES = K // (P * PACK)
 VB = T // P
 WINDOW = 704
+HALF = H // 2
 
 FLOPS = 2 * K * H * T * 2 + 2 * H * H * T
 
@@ -22,6 +24,7 @@ FP4X4 = mybir.dt.float4_e2m1fn_x4
 SILU = mybir.ActivationFunctionType.Silu
 MAX = mybir.AluOpType.max
 ADD = mybir.AluOpType.add
+MULT = mybir.AluOpType.mult
 
 
 def tile_picked_wedgecv_silu_lo_kernel(tc, x_words, x_scales, w1, w2, w3, pos1, pos2, pos3, pos4, out_0, out_1, out_2):
@@ -36,237 +39,299 @@ def tile_picked_wedgecv_silu_lo_kernel(tc, x_words, x_scales, w1, w2, w3, pos1, 
         lists = [sb("list%d" % d, [P, T // 16], U16) for d in range(D)]
         xw = sb("xw", [P, PASSES, 2 * T], U8)
         xs = sb("xs", [P, PASSES, T], U8)
+        ident = sb("ident", [P, P], F32)
         zeros = sb("zeros", [P, WINDOW - T], F32)
         e_win = [sb("e%d" % t, [P, WINDOW], F32) for t in range(PACK)]
         y_sb = [sb("y%d" % t, [P, T], F32) for t in range(PACK)]
+        banks = [psum.tile([P, T], F32, name="bank%d" % i) for i in range(8)]
 
         nc.gpsimd.memset(xs[:].bitcast(I32), 0)
         for q in range(4):
-            nc.sync.dma_start(
+            nc.scalar.dma_start(
                 xs[32 * q : 32 * q + 4, :, :].bitcast(I32),
                 x_scales[:, 4 * q : 4 * q + 4, :].rearrange("z r c -> r z c").bitcast(I32),
             )
         nc.gpsimd.memset(zeros[:], 0.0)
+        make_identity(nc, ident[:])
         for t in range(PACK):
             nc.scalar.activation(e_win[t][:, T:], zeros[:], SILU)
 
         raw = {}
+        rawt = {}
 
-        def load_w(m, w, z):
-            raw[(m, z)] = sb("raw%d_%d" % (m, z), [P, PACK, H], F32)
-            nc.sync.dma_start(raw[(m, z)][:], w[z * 512 : (z + 1) * 512, :].rearrange("(p j) c -> p j c", j=PACK))
+        def load_w(m, w, z, halves):
+            n = len(halves) * HALF
+            c0 = halves[0] * HALF
+            tl = sb("raw%d_%d_%d" % (m, z, halves[0]), [P, PACK, n], F32)
+            nc.sync.dma_start(tl[:], w[z * 512 : (z + 1) * 512, c0 : c0 + n].rearrange("(p j) c -> p j c", j=PACK))
+            rawt[(m, z, halves[0])] = tl[:].rearrange("p j c -> p (j c)")[:, :T]
+            for i, h in enumerate(halves):
+                raw[(m, z, h)] = tl[:, :, i * HALF : (i + 1) * HALF].rearrange("p j (c t) -> p c j t", t=PACK)
+            if len(halves) == 2:
+                raw[(m, z)] = tl[:].rearrange("p j (c t) -> p c j t", t=PACK)
 
-        load_w(0, w2, 0)
-        load_w(0, w2, 1)
-        nc.sync.dma_start(xw[:].bitcast(I32), x_words.rearrange("z p b -> p z b").bitcast(I32))
-        nc.sync.dma_start(lists[0][:], pos1)
-        load_w(1, w1, 0)
-        nc.sync.dma_start(lists[1][:], pos2)
-        load_w(1, w1, 1)
-        for tl, src in zip(lists[2:], (pos3, pos4)):
-            nc.sync.dma_start(tl[:], src)
-        load_w(2, w3, 0)
+        def load_x():
+            nc.sync.dma_start(xw[:].bitcast(I32), x_words.rearrange("z p b -> p z b").bitcast(I32))
 
-        banks = [psum.tile([P, T], F32, name="bank%d" % i) for i in range(4)]
-        wq = {}
+        def load_list(d):
+            nc.sync.dma_start(lists[d][:], (pos1, pos2, pos3, pos4)[d])
+
+        load_w(0, w2, 0, (0,))
+        load_w(0, w2, 1, (0,))
+        load_x()
+        load_list(0)
+        load_w(0, w2, 0, (1,))
+        load_list(1)
+        load_w(0, w2, 1, (1,))
+        load_list(2)
+        load_w(1, w1, 0, (0, 1))
+        load_list(3)
+        load_w(1, w1, 1, (0, 1))
+        load_w(2, w3, 0, (0, 1))
+
         stage = {}
+        wq = {}
 
-        def prep(m, z, h, eng):
-            stage[(m, z, h)] = sb("wb%d_%d_%d" % (m, z, h), [P, T], F32)
-            wb = stage[(m, z, h)][:].bitcast(BF16)
-            codes = sb("wc%d_%d_%d" % (m, z, h), [P, 2 * P], U32)
-            scales = sb("ws%d_%d_%d" % (m, z, h), [P, 2 * P], U8)
-            wq[(m, z, h)] = (codes, scales)
-            dst = wb.rearrange("p (t c j) -> p c j t", t=2, j=PACK)
-            src = raw[(m, z)][:].rearrange("p j (c t) -> p c j t", t=PACK)[:, :, :, 2 * h : 2 * h + 2]
+        def staging(key):
+            if key not in stage:
+                name = "_".join(str(k) for k in key)
+                stage[key] = sb("wb" + name, [P, T], F32)
+                wq[key] = (sb("wc" + name, [P, 2 * P], U32), sb("ws" + name, [P, 2 * P], U8))
+            return stage[key][:].bitcast(BF16)
+
+        def cast(dst, src, eng):
             if eng == "v":
                 nc.vector.tensor_copy(dst, src)
             elif eng == "g":
-                nc.gpsimd.tensor_copy(dst, src)
+                nc.gpsimd.tensor_scalar(dst, src, 1.0, 0.0, MULT, ADD)
             else:
                 nc.scalar.copy(dst, src)
-            nc.vector.quantize_mx(codes[:].bitcast(FP8X4), scales[:], wb)
+
+        def cast_a(m, h, z, eng):
+            dst = staging((m, "a", h))[:, z * 512 : (z + 1) * 512].rearrange("p (c e j) -> p c j e", e=2, j=PACK)
+            cast(dst, raw[(m, z, h)][:, :, :, 0:2], eng)
+
+        def cast_b(m, z, eng, h=None, pair=1):
+            dst = staging((m, "b", z, pair)).rearrange("p (t c j) -> p c j t", t=2, j=PACK)
+            if h is None:
+                cast(dst, raw[(m, z)][:, :, :, 2 * pair : 2 * pair + 2], eng)
+            else:
+                cast(dst[:, 64 * h : 64 * h + 64], raw[(m, z, h)][:, :, :, 2 * pair : 2 * pair + 2], eng)
+
+        def quant(key, z=None):
+            codes, scales = wq[key]
+            if z is None:
+                nc.vector.quantize_mx(codes[:].bitcast(FP8X4), scales[:], staging(key))
+            else:
+                cols = slice(z * P, (z + 1) * P)
+                nc.vector.quantize_mx(codes[:, cols].bitcast(FP8X4), scales[:, cols], staging(key)[:, z * 512 : (z + 1) * 512])
 
         def project(m, t, b):
             acc = banks[b]
-            cols = slice((t % 2) * P, (t % 2 + 1) * P)
             for z in range(PASSES):
-                codes, scales = wq[(m, z, t // 2)]
+                codes, scales = wq[(m, "a", t)] if t < 2 else wq[(m, "b", z, 1)]
+                i = z if t < 2 else t - 2
+                cols = slice(i * P, (i + 1) * P)
                 nc.tensor.matmul_mx(
                     acc[:], lhsT=codes[:, cols].bitcast(FP8X4), lhsT_scale=scales[:, cols],
                     rhs=xw[:, z, :].bitcast(FP4X4), rhs_scale=xs[:, z, :], start=z == 0, stop=z == PASSES - 1,
                 )
             nc.scalar.copy(e_win[t][:, :T] if m == 0 else y_sb[t][:], acc[:])
 
-        ua = [sb("ua%d" % d, [P, 2, T], F32) for d in range(D)]
-        ub = {}
-        mid = {}
-
-        def sums(t, d, v0, n):
-            return ua[d][:, t, v0 : v0 + n] if t < 2 else ub[(v0, d)][:, t - 2, :]
         early = {}
 
         def window(t, d, v0, n):
             return e_win[t][:].indirect(lists[d][:, v0 // 16 : (v0 + n) // 16])
 
-        def fetch(t, d, held=None):
-            early[(t, d)] = sb("g%d_%d" % (t, d), [P, T], F32) if held is None else stage[held]
-            nc.vector.tensor_copy(early[(t, d)][:], window(t, d, 0, T))
+        def fetch(h, d, held=None):
+            early[(h, d)] = sb("g%d_%d" % (h, d), [P, T], F32) if held is None else stage[held] if held in stage else rawt[held]
+            nc.vector.tensor_copy(early[(h, d)][:], window(h, d, 0, T))
 
-        def centre(t, d, v0=0, n=T):
-            nc.vector.tensor_tensor(sums(t, d, v0, n), early[(t, d)][:, v0 : v0 + n], y_sb[t][:, v0 : v0 + n], ADD)
+        act = [sb("act%d" % vb, [P, D, 2, 2 * P], BF16) for vb in range(VB)]
+        best = [sb("best%d" % vb, [P, 3, P], F32) for vb in range(VB)]
+        zb = [sb("zb%d" % vb, [P, P, 2], F32) for vb in range(VB)]
+        ub = {}
+        part = {}
+        obs = {}
 
-        def fused(t, d, v0=0, n=T):
-            nc.vector.tensor_tensor(sums(t, d, v0, n), window(t, d, v0, n), y_sb[t][:, v0 : v0 + n], ADD)
+        def edge_a(h, vb, b):
+            bank = banks[b][:].rearrange("v (d c) -> v d c", d=D)
+            cols = slice(vb * P, (vb + 1) * P)
+            steps = [(d, y_sb[h][:, cols]) for d in range(D)] + [(d, early[(h, d)][:, cols]) for d in range(D)]
+            for i, (d, src) in enumerate(steps):
+                nc.tensor.matmul(bank[:, d, :], lhsT=src, rhs=ident[:], start=i == 0, stop=i == len(steps) - 1, is_transpose=True)
+            nc.scalar.activation(act[vb][:, :, 1, h * P : (h + 1) * P], bank, SILU)
+
+        def pool(vb, r0=0):
+            m = sb("m%d" % vb, [P, 2, 2 - r0, 2 * P], BF16)
+            nc.vector.tensor_tensor(m[:], act[vb][:, 0:2, r0:, :], act[vb][:, 2:4, r0:, :], MAX)
+            nc.vector.tensor_tensor(best[vb][:, 1 + r0 :, :].bitcast(BF16), m[:, 0], m[:, 1], MAX)
+
+        def back_a(vb, b):
+            nc.tensor.transpose(banks[b][:, :P], best[vb][:, 2, :], ident[:])
+            nc.scalar.copy(best[vb][:, 0, :], banks[b][:, :P])
+
+        def piece(vb, ds=range(D)):
+            for d in ds:
+                old = vb - 2 + d // 2
+                if old < 0:
+                    ub[(vb, d)] = sb("ub%d_%d" % (vb, d), [P, 2, P], F32)[:]
+                else:
+                    ub[(vb, d)] = act[old][:, d].rearrange("p r n -> p (r n)").bitcast(F32).rearrange("p (t v) -> p t v", t=2)
+                for t in (2, 3):
+                    nc.vector.tensor_tensor(ub[(vb, d)][:, t - 2, :], window(t, d, vb * P, P), y_sb[t][:, vb * P : (vb + 1) * P], ADD)
+                nc.scalar.activation(act[vb][:, d, 0, :].rearrange("p (v t) -> p v t", t=2), ub[(vb, d)].rearrange("p t v -> p v t"), SILU)
+
+        def pool_step(vb, d):
+            dst = sb("mp%d_%d" % (vb, d), [P, 2 * P], BF16)[:] if d < D - 1 else best[vb][:, 1, :].bitcast(BF16)
+            nc.vector.tensor_tensor(dst, act[vb][:, 0, 0, :] if d == 1 else part[vb], act[vb][:, d, 0, :], MAX)
+            part[vb] = dst
+
+        def weave(vb, eng="s"):
+            src = best[vb][:, 0:2, :].rearrange("p h v -> p v h")
+            if eng == "s":
+                nc.scalar.copy(zb[vb][:], src)
+            else:
+                nc.vector.tensor_copy(zb[vb][:], src)
 
         oc = sb("oc", [P, T], U32)
         os_ = sb("os", [P, T], U8)
         out_rows = out_0.rearrange("(p t) v -> p t v", t=PACK)
         out_words = out_1[0].rearrange("p c r -> p (c r)").bitcast(I32)
-        s = {}
-        zb = {}
-        obs = {}
 
-        best = sb("best", [P, 2, 2 * T], BF16)
-        part = {}
-
-        def act(h, d, v0, n):
-            if (h, v0) not in s:
-                s[(h, v0)] = sb("s%d_%d" % (h, v0), [P, D, n, 2], BF16)
-            nc.scalar.activation(s[(h, v0)][:, d], (ua[d][:, :, v0 : v0 + n] if h == 0 else ub[(v0, d)]).rearrange("p t v -> p v t"), SILU)
-
-        def pool(h, v0, n):
-            m = sb("m%d_%d" % (h, v0), [P, 2, 2 * n], BF16)
-            mid[(h, v0)] = m
-            src = s[(h, v0)][:].rearrange("p d v t -> p d (v t)")
-            nc.vector.tensor_tensor(m[:], src[:, 0:2, :], src[:, 2:4, :], MAX)
-            nc.vector.tensor_tensor(best[:, h, 2 * v0 : 2 * (v0 + n)], m[:, 0, :], m[:, 1, :], MAX)
-
-        def pool_step(h, v0, n, d):
-            src = s[(h, v0)][:].rearrange("p d v t -> p d (v t)")
-            dst = sb("mp%d_%d" % (v0, d), [P, 2 * n], BF16)[:] if d < D - 1 else best[:, h, 2 * v0 : 2 * (v0 + n)]
-            nc.vector.tensor_tensor(dst, src[:, 0, :] if d == 1 else part[v0], src[:, d, :], MAX)
-            part[v0] = dst
-
-        def weave(v0, n, eng="s"):
-            zb[v0] = sb("zb%d" % v0, [P, n * PACK], BF16)
-            dst = zb[v0][:].bitcast(F32).rearrange("p (v h) -> p v h", h=2)
-            src = best[:].bitcast(F32)[:, :, v0 : v0 + n].rearrange("p h v -> p v h")
-            if eng == "s":
-                nc.scalar.copy(dst, src)
-            else:
-                nc.vector.tensor_copy(dst, src)
-
-        def result(v0, n, how):
-            cols = slice(v0, v0 + n)
-            zc = sb("zc%d" % v0, [P, n], U32)
-            zs = sb("zs%d" % v0, [P, n], U8)
-            nc.vector.quantize_mx(zc[:].bitcast(FP8X4), zs[:], zb[v0][:])
-            acc = psum.tile([P, PACK, n], F32, name="res", tag="res", bufs=4)
+        def result(vb, how, b):
+            cols = slice(vb * P, (vb + 1) * P)
+            zc = sb("zc%d" % vb, [P, P], U32)
+            zs = sb("zs%d" % vb, [P, P], U8)
+            nc.vector.quantize_mx(zc[:].bitcast(FP8X4), zs[:], zb[vb][:].rearrange("p v h -> p (v h)").bitcast(BF16))
+            acc = banks[b][:].rearrange("p (t v) -> p t v", t=PACK)
             for t in range(PACK):
-                codes, scales = wq[(2, 0, t // 2)]
+                codes, scales = wq[(2, "b", 0, t // 2)]
                 tc_ = slice((t % 2) * P, (t % 2 + 1) * P)
                 nc.tensor.matmul_mx(
                     acc[:, t, :], lhsT=codes[:, tc_].bitcast(FP8X4), lhsT_scale=scales[:, tc_],
                     rhs=zc[:].bitcast(FP8X4), rhs_scale=zs[:], start=True, stop=True,
                 )
-            o32 = sb("o32_%d" % v0, [P, PACK, n], F32)
-            ob = sb("ob%d" % v0, [P, n, PACK], BF16)
+            o32 = sb("o32_%d" % vb, [P, PACK, P], F32)
+            ob = sb("ob%d" % vb, [P, P, PACK], BF16)
             if how == "p":
-                nc.vector.tensor_copy(ob[:], acc[:].rearrange("p t v -> p v t"))
+                nc.vector.tensor_copy(ob[:], acc.rearrange("p t v -> p v t"))
             elif how == "s":
-                nc.scalar.copy(ob[:], acc[:].rearrange("p t v -> p v t"))
-            nc.scalar.copy(o32[:], acc[:])
+                nc.scalar.copy(ob[:], acc.rearrange("p t v -> p v t"))
+            nc.scalar.copy(o32[:], acc)
             nc.sync.dma_start(out_rows[:, :, cols], o32[:])
-            obs[v0] = ob
+            if how in "vg":
+                cast(ob[:].rearrange("p (c i) t -> p c t i", i=4), o32[:].rearrange("p t (c i) -> p c t i", i=4), how)
+            obs[vb] = ob
 
-        def planes(v0, n):
-            cols = slice(v0, v0 + n)
-            nc.vector.quantize_mx(oc[:, cols].bitcast(FP8X4), os_[:, cols], obs[v0][:].rearrange("p v t -> p (v t)"))
-            nc.sync.dma_start(out_words[:, cols], oc[:, cols].bitcast(I32))
-
-        def piece(v0, n, ds=range(D), held=None):
-            for d in ds:
-                if held is None:
-                    ub[(v0, d)] = sb("ub%d_%d" % (v0, d), [P, 2, n], F32)[:]
-                else:
-                    ub[(v0, d)] = held.bitcast(F32)[:, : 2 * n].rearrange("p (t v) -> p t v", t=2)
-                for t in (2, 3):
-                    fused(t, d, v0, n)
-                act(1, d, v0, n)
-
-        def last_result(v0, n):
-            cols = slice(v0, v0 + n)
-            zc = sb("zc%d" % v0, [P, n], U32)
-            zs = sb("zs%d" % v0, [P, n], U8)
-            nc.vector.quantize_mx(zc[:].bitcast(FP8X4), zs[:], zb[v0][:])
-            accs = [banks[h][:, : 2 * n].rearrange("p (t v) -> p t v", t=2) for h in range(2)]
+        def last_result(vb, b0, b1):
+            cols = slice(vb * P, (vb + 1) * P)
+            zc = sb("zc%d" % vb, [P, P], U32)
+            zs = sb("zs%d" % vb, [P, P], U8)
+            nc.vector.quantize_mx(zc[:].bitcast(FP8X4), zs[:], zb[vb][:].rearrange("p v h -> p (v h)").bitcast(BF16))
+            accs = [banks[b][:, : 2 * P].rearrange("p (t v) -> p t v", t=2) for b in (b0, b1)]
             for t in range(PACK):
-                codes, scales = wq[(2, 0, t // 2)]
+                codes, scales = wq[(2, "b", 0, t // 2)]
                 tc_ = slice((t % 2) * P, (t % 2 + 1) * P)
                 nc.tensor.matmul_mx(
                     accs[t // 2][:, t % 2, :], lhsT=codes[:, tc_].bitcast(FP8X4), lhsT_scale=scales[:, tc_],
                     rhs=zc[:].bitcast(FP8X4), rhs_scale=zs[:], start=True, stop=True,
                 )
-            o32 = sb("o32_%d" % v0, [P, PACK, n], F32)
-            ob = sb("ob%d" % v0, [P, n, PACK], BF16)
-            for h in range(2):
-                nc.scalar.copy(o32[:, 2 * h : 2 * h + 2, :], accs[h])
-            nc.sync.dma_start(out_rows[:, :, cols], o32[:])
-            nc.vector.tensor_copy(ob[:].rearrange("p (c i) t -> p c t i", i=4), o32[:].rearrange("p t (c i) -> p c t i", i=4))
-            obs[v0] = ob
+            o32 = sb("o32_%d" % vb, [P, PACK, P], F32)
+            ob = sb("ob%d" % vb, [P, P, PACK], BF16)
+            nc.scalar.copy(o32[:, 0:2, :], accs[0])
+            nc.vector.tensor_copy(o32[:, 2:4, :], accs[1])
+            nc.scalar.dma_start(out_rows[:, :, cols], o32[:])
+            cast(ob[:].rearrange("p (c i) t -> p c t i", i=4), o32[:].rearrange("p t (c i) -> p c t i", i=4), "v")
+            obs[vb] = ob
 
-        prep(0, 0, 0, "v")
-        prep(0, 0, 1, "v")
-        prep(0, 1, 0, "v")
+        def planes(vb):
+            cols = slice(vb * P, (vb + 1) * P)
+            nc.vector.quantize_mx(oc[:, cols].bitcast(FP8X4), os_[:, cols], obs[vb][:].rearrange("p v t -> p (v t)"))
+            nc.sync.dma_start(out_words[:, cols], oc[:, cols].bitcast(I32))
+
+        cast_a(0, 0, 0, "v")
+        quant((0, "a", 0), 0)
+        cast_b(0, 0, "s", 0)
+        cast_a(0, 0, 1, "v")
+        quant((0, "a", 0), 1)
+        cast_b(0, 1, "s", 0)
         project(0, 0, 0)
+        cast_a(0, 1, 0, "v")
         fetch(0, 0)
-        prep(0, 1, 1, "s")
+        cast_a(0, 1, 1, "s")
+        quant((0, "a", 1))
+        fetch(0, 1, (0, "a", 1))
+        cast_b(0, 0, "s", 1)
+        cast_b(0, 1, "s", 1)
         project(0, 1, 1)
-        prep(1, 0, 0, "s")
-        fetch(0, 1)
-        prep(1, 1, 0, "v")
-        fetch(0, 2, (1, 1, 0))
-        fetch(0, 3, (1, 0, 0))
-        project(1, 1, 0)
-        project(1, 0, 1)
-        prep(1, 0, 1, "s")
-        prep(1, 1, 1, "s")
+        fetch(0, 2, (0, 1, 1))
+        quant((0, "b", 1, 1))
+        fetch(0, 3, (0, "b", 1, 1))
+        quant((0, "b", 0, 1))
+        cast_a(1, 0, 0, "s")
+        cast_a(1, 1, 0, "s")
+        cast_b(1, 0, "s")
+        fetch(1, 0, (0, "b", 0, 1))
+        cast_a(1, 0, 1, "s")
+        quant((1, "a", 0))
+        quant((1, "b", 0, 1))
+        fetch(1, 1, (1, "a", 0))
+        cast_a(1, 1, 1, "s")
+        cast_b(1, 1, "s")
+        project(1, 0, 0)
+        quant((1, "a", 1))
+        quant((1, "b", 1, 1))
+        fetch(1, 2, (1, "b", 1, 1))
+        fetch(1, 3, (1, 1, 0))
         project(0, 2, 0)
-        project(0, 3, 1)
         project(1, 2, 2)
+        project(0, 3, 1)
         project(1, 3, 3)
-        prep(2, 0, 0, "s")
-        for d in range(D):
-            fused(1, d)
-            centre(0, d)
-            act(0, d, 0, T)
-        prep(2, 0, 1, "s")
-        piece(0, P)
-        pool(0, 0, T)
-        pool(1, 0, P)
-        weave(0, P)
-        result(0, P, "s")
-        piece(P, P)
-        planes(0, P)
-        pool(1, P, P)
-        weave(P, P)
-        result(P, P, "s")
-        piece(2 * P, P)
-        planes(P, P)
-        pool(1, 2 * P, P)
-        weave(2 * P, P)
-        result(2 * P, P, "s")
-        piece(3 * P, P, range(2))
-        pool_step(1, 3 * P, P, 1)
-        piece(3 * P, P, range(2, 3))
-        planes(2 * P, P)
-        pool_step(1, 3 * P, P, 2)
-        piece(3 * P, P, range(3, 4))
-        pool_step(1, 3 * P, P, 3)
-        weave(3 * P, P, "v")
-        result(3 * P, P, "p")
-        planes(3 * P, P)
+        project(1, 1, 6)
+        edge_a(0, 0, 4)
+        cast_b(2, 0, "s", None, 0)
+        edge_a(1, 0, 5)
+        piece(0)
+        edge_a(0, 1, 4)
+        piece(1, range(2))
+        pool(0)
+        back_a(0, 1)
+        edge_a(1, 1, 5)
+        cast_b(2, 0, "s", None, 1)
+        quant((2, "b", 0, 0))
+        quant((2, "b", 0, 1))
+        weave(0)
+        piece(1, range(2, 4))
+        edge_a(0, 2, 4)
+        piece(2, range(2))
+        pool(1)
+        result(0, "s", 6)
+        back_a(1, 1)
+        edge_a(1, 2, 5)
+        weave(1)
+        piece(2, range(2, 4))
+        planes(0)
+        edge_a(0, 3, 4)
+        edge_a(1, 3, 5)
+        piece(3, range(2))
+        pool(2)
+        result(1, "s", 7)
+        back_a(2, 1)
+        pool(3, 1)
+        weave(2)
+        pool_step(3, 1)
+        piece(3, range(2, 3))
+        planes(1)
+        result(2, "s", 6)
+        piece(3, range(3, 4))
+        back_a(3, 2)
+        pool_step(3, 2)
+        pool_step(3, 3)
+        weave(3, "v")
+        planes(2)
+        last_result(3, 7, 0)
+        planes(3)
         for q in range(4):
             eng = nc.sync if q % 2 == 0 else nc.scalar
             eng.dma_start(out_2[0, 4 * q : 4 * q + 4, :].bitcast(I32), os_[32 * q : 32 * q + 4, :].bitcast(I32))

@@ -108,7 +108,7 @@ def tile_picked_wedgecv_silu_lo_kernel(tc, x_words, x_scales, w1, w2, w3, pos1, 
                 nc.scalar.copy(dst, src)
 
         def cast_a(m, h, z, eng):
-            dst = staging((m, "a", h))[:, z * 512 : (z + 1) * 512].rearrange("p (c e j) -> p c j e", e=2, j=PACK)
+            dst = staging((m, "a", h))[:, z * 512 : (z + 1) * 512].rearrange("p (e c j) -> p c j e", e=2, j=PACK)
             cast(dst, raw[(m, z, h)][:, :, :, 0:2], eng)
 
         def cast_b(m, z, eng, h=None, pair=1):
@@ -125,6 +125,32 @@ def tile_picked_wedgecv_silu_lo_kernel(tc, x_words, x_scales, w1, w2, w3, pos1, 
             else:
                 cols = slice(z * P, (z + 1) * P)
                 nc.vector.quantize_mx(codes[:, cols].bitcast(FP8X4), scales[:, cols], staging(key)[:, z * 512 : (z + 1) * 512])
+
+        wide = {}
+
+        def cast_all(m, z, h, eng):
+            if (m, z) not in wide:
+                stage[(m, z, 0)] = sb("wide%d_%d" % (m, z), [P, 2 * T], F32)
+                wide[(m, z)] = stage[(m, z, 0)][:].bitcast(BF16).rearrange("p (t c j) -> p t c j", t=PACK, j=PACK)
+                stage[(m, z, 1)] = stage[(m, z, 0)][:, T:]
+                stage[(m, z, 0)] = stage[(m, z, 0)][:, :T]
+            cast(wide[(m, z)][:, :, 64 * h : 64 * h + 64, :].rearrange("p t c j -> p c j t"), raw[(m, z, h)], eng)
+
+        def operand(key):
+            if key not in wq:
+                name = "_".join(str(k) for k in key)
+                wq[key] = (sb("wc" + name, [P, 2 * P], U32), sb("ws" + name, [P, 2 * P], U8))
+            return wq[key]
+
+        def quant_a(m, h, z):
+            codes, scales = operand((m, "a", h))
+            for e in range(2):
+                cols = slice(z * P + 64 * e, z * P + 64 * e + 64)
+                nc.vector.quantize_mx(codes[:, cols].bitcast(FP8X4), scales[:, cols], wide[(m, z)][:, e, 64 * h : 64 * h + 64, :].rearrange("p c j -> p (c j)"))
+
+        def quant_b(m, z, pair=1):
+            codes, scales = operand((m, "b", z, pair))
+            nc.vector.quantize_mx(codes[:].bitcast(FP8X4), scales[:], wide[(m, z)][:, 2 * pair : 2 * pair + 2].rearrange("p t c j -> p (t c j)"))
 
         def project(m, t, b):
             acc = banks[b]
@@ -144,7 +170,7 @@ def tile_picked_wedgecv_silu_lo_kernel(tc, x_words, x_scales, w1, w2, w3, pos1, 
             return e_win[t][:].indirect(lists[d][:, v0 // 16 : (v0 + n) // 16])
 
         def fetch(h, d, held=None):
-            early[(h, d)] = sb("g%d_%d" % (h, d), [P, T], F32) if held is None else stage[held] if held in stage else rawt[held]
+            early[(h, d)] = sb("g%d_%d" % (h, d), [P, T], F32) if held is None else rawt[held[1:]] if held[0] == "raw" else stage[held]
             nc.vector.tensor_copy(early[(h, d)][:], window(h, d, 0, T))
 
         act = [sb("act%d" % vb, [P, D, 2, 2 * P], BF16) for vb in range(VB)]
@@ -160,7 +186,7 @@ def tile_picked_wedgecv_silu_lo_kernel(tc, x_words, x_scales, w1, w2, w3, pos1, 
             steps = [(d, y_sb[h][:, cols]) for d in range(D)] + [(d, early[(h, d)][:, cols]) for d in range(D)]
             for i, (d, src) in enumerate(steps):
                 nc.tensor.matmul(bank[:, d, :], lhsT=src, rhs=ident[:], start=i == 0, stop=i == len(steps) - 1, is_transpose=True)
-            nc.scalar.activation(act[vb][:, :, 1, h * P : (h + 1) * P], bank, SILU)
+            nc.scalar.activation(act[vb][:, :, 1, h * P : (h + 1) * P].rearrange("v d (c e) -> v d c e", e=2), bank.rearrange("v d (e c) -> v d c e", e=2), SILU)
 
         def pool(vb, r0=0):
             m = sb("m%d" % vb, [P, 2, 2 - r0, 2 * P], BF16)
@@ -265,24 +291,24 @@ def tile_picked_wedgecv_silu_lo_kernel(tc, x_words, x_scales, w1, w2, w3, pos1, 
         cast_b(0, 0, "s", 1)
         cast_b(0, 1, "s", 1)
         project(0, 1, 1)
-        fetch(0, 2, (0, 1, 1))
+        fetch(0, 2, ("raw", 0, 1, 1))
         quant((0, "b", 1, 1))
         fetch(0, 3, (0, "b", 1, 1))
         quant((0, "b", 0, 1))
-        cast_a(1, 0, 0, "s")
-        cast_a(1, 1, 0, "s")
-        cast_b(1, 0, "s")
+        cast_all(1, 0, 0, "s")
+        cast_all(1, 0, 1, "s")
         fetch(1, 0, (0, "b", 0, 1))
-        cast_a(1, 0, 1, "s")
-        quant((1, "a", 0))
-        quant((1, "b", 0, 1))
-        fetch(1, 1, (1, "a", 0))
-        cast_a(1, 1, 1, "s")
-        cast_b(1, 1, "s")
+        cast_all(1, 1, 0, "s")
+        quant_a(1, 0, 0)
+        quant_a(1, 1, 0)
+        quant_b(1, 0)
+        quant_a(1, 0, 1)
+        fetch(1, 1, (1, 0, 0))
+        cast_all(1, 1, 1, "s")
         project(1, 0, 0)
-        quant((1, "a", 1))
-        quant((1, "b", 1, 1))
-        fetch(1, 2, (1, "b", 1, 1))
+        quant_a(1, 1, 1)
+        quant_b(1, 1)
+        fetch(1, 2, (1, 1, 1))
         fetch(1, 3, (1, 1, 0))
         project(0, 2, 0)
         project(1, 2, 2)
@@ -290,7 +316,7 @@ def tile_picked_wedgecv_silu_lo_kernel(tc, x_words, x_scales, w1, w2, w3, pos1, 
         project(1, 3, 3)
         project(1, 1, 6)
         edge_a(0, 0, 4)
-        cast_b(2, 0, "s", None, 0)
+        cast_all(2, 0, 0, "s")
         edge_a(1, 0, 5)
         piece(0)
         edge_a(0, 1, 4)
@@ -298,9 +324,9 @@ def tile_picked_wedgecv_silu_lo_kernel(tc, x_words, x_scales, w1, w2, w3, pos1, 
         pool(0)
         back_a(0, 1)
         edge_a(1, 1, 5)
-        cast_b(2, 0, "s", None, 1)
-        quant((2, "b", 0, 0))
-        quant((2, "b", 0, 1))
+        cast_all(2, 0, 1, "s")
+        quant_b(2, 0, 0)
+        quant_b(2, 0, 1)
         weave(0)
         piece(1, range(2, 4))
         edge_a(0, 2, 4)

@@ -7,9 +7,9 @@ K, T, H, D = 1024, 512, 512, 4
 P = 128
 PACK = 4
 PASSES = K // (P * PACK)
-VB = T // P
-WINDOW = 704
+BLOCKS = T // P
 HALF = H // 2
+WIDE = 704
 
 FLOPS = 2 * K * H * T * 2 + 2 * H * H * T
 
@@ -24,340 +24,287 @@ FP4X4 = mybir.dt.float4_e2m1fn_x4
 SILU = mybir.ActivationFunctionType.Silu
 MAX = mybir.AluOpType.max
 ADD = mybir.AluOpType.add
-MULT = mybir.AluOpType.mult
 
 
-def tile_picked_wedgecv_silu_lo_kernel(tc, x_words, x_scales, w1, w2, w3, pos1, pos2, pos3, pos4, out_0, out_1, out_2):
+def tile_picked_wedgecv_silu_lo_kernel(
+    tc, x_words, x_scales, w1, w2, w3, pos1, pos2, pos3, pos4, out_0, out_1, out_2
+):
     nc = tc.nc
     with ExitStack() as ctx:
         keep = ctx.enter_context(tc.tile_pool(name="keep", bufs=1))
         psum = ctx.enter_context(tc.psum_pool(name="psum", bufs=1))
 
-        def sb(name, shape, dtype):
-            return keep.tile(shape, dtype, name=name, align_bytes=64)
+        def sb(name, shape, dtype, tag=None):
+            return keep.tile(shape, dtype, name=name, tag=tag or name, align_bytes=64)
+
+        def mx_tiles(name, columns):
+            return sb(name + "_codes", [P, columns], U32), sb(name + "_scales", [P, columns], U8)
+
+        def quantise(operand, first, values):
+            cols = slice(first, first + values.shape[1] // PACK)
+            nc.vector.quantize_mx(operand[0][:, cols].bitcast(FP8X4), operand[1][:, cols], values)
+
+        def as_sums(view):
+            return view.bitcast(F32)[:, :T]
 
         lists = [sb("list%d" % d, [P, T // 16], U16) for d in range(D)]
         xw = sb("xw", [P, PASSES, 2 * T], U8)
         xs = sb("xs", [P, PASSES, T], U8)
         ident = sb("ident", [P, P], F32)
-        zeros = sb("zeros", [P, WINDOW - T], F32)
-        e_win = [sb("e%d" % t, [P, WINDOW], F32) for t in range(PACK)]
+        zeros = sb("zeros", [P, WIDE - T], F32)
+        e_sb = [sb("e%d" % h, [P, WIDE], F32) for h in range(2)]
         y_sb = [sb("y%d" % t, [P, T], F32) for t in range(PACK)]
-        banks = [psum.tile([P, T], F32, name="bank%d" % i) for i in range(8)]
+        banks = [psum.tile([P, T], F32, name="bank%d" % b) for b in range(8)]
 
         nc.gpsimd.memset(xs[:].bitcast(I32), 0)
         for q in range(4):
             nc.scalar.dma_start(
                 xs[32 * q : 32 * q + 4, :, :].bitcast(I32),
-                x_scales[:, 4 * q : 4 * q + 4, :].rearrange("z r c -> r z c").bitcast(I32),
+                x_scales[:, 4 * q : 4 * q + 4, :].rearrange("g r c -> r g c").bitcast(I32),
             )
         nc.gpsimd.memset(zeros[:], 0.0)
         make_identity(nc, ident[:])
-        for t in range(PACK):
-            nc.scalar.activation(e_win[t][:, T:], zeros[:], SILU)
+        for h in range(2):
+            nc.scalar.activation(e_sb[h][:, T:], zeros[:], SILU)
 
-        raw = {}
-        rawt = {}
-
-        def load_w(m, w, z, halves):
-            n = len(halves) * HALF
-            c0 = halves[0] * HALF
-            tl = sb("raw%d_%d_%d" % (m, z, halves[0]), [P, PACK, n], F32)
-            nc.sync.dma_start(tl[:], w[z * 512 : (z + 1) * 512, c0 : c0 + n].rearrange("(p j) c -> p j c", j=PACK))
-            rawt[(m, z, halves[0])] = tl[:].rearrange("p j c -> p (j c)")[:, :T]
-            for i, h in enumerate(halves):
-                raw[(m, z, h)] = tl[:, :, i * HALF : (i + 1) * HALF].rearrange("p j (c t) -> p c j t", t=PACK)
-            if len(halves) == 2:
-                raw[(m, z)] = tl[:].rearrange("p j (c t) -> p c j t", t=PACK)
-
-        def load_x():
-            nc.sync.dma_start(xw[:].bitcast(I32), x_words.rearrange("z p b -> p z b").bitcast(I32))
+        def load_rows(name, w, g, first, columns):
+            rows = sb(name, [P, PACK, columns], F32)
+            nc.sync.dma_start(
+                rows[:], w[g * P * PACK : (g + 1) * P * PACK, first : first + columns].rearrange("(p j) c -> p j c", j=PACK)
+            )
+            return rows
 
         def load_list(d):
             nc.sync.dma_start(lists[d][:], (pos1, pos2, pos3, pos4)[d])
 
-        load_w(0, w2, 0, (0,))
-        load_w(0, w2, 1, (0,))
-        load_x()
+        w2_in = [[load_rows("w2_0%d" % g, w2, g, 0, HALF) for g in range(PASSES)]]
+        nc.sync.dma_start(xw[:].bitcast(I32), x_words.rearrange("g p b -> p g b").bitcast(I32))
         load_list(0)
-        load_w(0, w2, 0, (1,))
+        w2_in.append([load_rows("w2_10", w2, 0, HALF, HALF)])
         load_list(1)
-        load_w(0, w2, 1, (1,))
+        w2_in[1].append(load_rows("w2_11", w2, 1, HALF, HALF))
+        w1_first = [load_rows("w1_00", w1, 0, 0, HALF)]
         load_list(2)
-        load_w(1, w1, 0, (0, 1))
+        w1_first.append(load_rows("w1_01", w1, 0, HALF, HALF))
         load_list(3)
-        load_w(1, w1, 1, (0, 1))
-        load_w(2, w3, 0, (0, 1))
+        w1_second = load_rows("w1_1", w1, 1, 0, H)
+        w3_in = load_rows("w3_in", w3, 0, 0, H)
 
-        stage = {}
-        wq = {}
+        e_sb.append(sb("e2", [P, T], F32, "w1_01"))
+        e_sb.append(sb("e3", [P, T], F32))
 
-        def staging(key):
-            if key not in stage:
-                name = "_".join(str(k) for k in key)
-                stage[key] = sb("wb" + name, [P, T], F32)
-                wq[key] = (sb("wc" + name, [P, 2 * P], U32), sb("ws" + name, [P, 2 * P], U8))
-            return stage[key][:].bitcast(BF16)
+        def by_word(rows):
+            return rows.rearrange("p j (c t) -> p c j t", t=PACK)
 
-        def cast(dst, src, eng):
-            if eng == "v":
-                nc.vector.tensor_copy(dst, src)
-            elif eng == "g":
-                nc.gpsimd.tensor_scalar(dst, src, 1.0, 0.0, MULT, ADD)
-            else:
-                nc.scalar.copy(dst, src)
+        w2_turned = [sb("w2_turned%d" % h, [P, PASSES, 2, HALF // PACK, PACK], BF16) for h in range(2)]
+        w2_direct = [sb("w2_direct%d" % g, [P, 2, P, PACK], BF16) for g in range(PASSES)]
+        w1_round = [sb("w1_round%d" % g, [P, PACK, P, PACK], BF16) for g in range(PASSES)]
+        w3_round = sb("w3_round", [P, PACK, P, PACK], BF16)
+        turned = [[mx_tiles("turned%d%d" % (m, h), PASSES * P) for h in range(2)] for m in range(2)]
+        direct = [[mx_tiles("direct%d%d" % (m, g), 2 * P) for g in range(PASSES)] for m in range(2)]
+        w3_mx = [mx_tiles("w3_mx%d" % u, 2 * P) for u in range(2)]
 
-        def cast_a(m, h, z, eng):
-            dst = staging((m, "a", h))[:, z * 512 : (z + 1) * 512].rearrange("p (e c j) -> p c j e", e=2, j=PACK)
-            cast(dst, raw[(m, z, h)][:, :, :, 0:2], eng)
+        def half_columns(h):
+            return slice(h * HALF // PACK, (h + 1) * HALF // PACK)
 
-        def cast_b(m, z, eng, h=None, pair=1):
-            dst = staging((m, "b", z, pair)).rearrange("p (t c j) -> p c j t", t=2, j=PACK)
-            if h is None:
-                cast(dst, raw[(m, z)][:, :, :, 2 * pair : 2 * pair + 2], eng)
-            else:
-                cast(dst[:, 64 * h : 64 * h + 64], raw[(m, z, h)][:, :, :, 2 * pair : 2 * pair + 2], eng)
+        def round_w2_turned(h, g, copy):
+            copy(w2_turned[h][:, g].rearrange("p t c j -> p c j t"), by_word(w2_in[h][g][:])[:, :, :, 0:2])
 
-        def quant(key, z=None):
-            codes, scales = wq[key]
-            if z is None:
-                nc.vector.quantize_mx(codes[:].bitcast(FP8X4), scales[:], staging(key))
-            else:
-                cols = slice(z * P, (z + 1) * P)
-                nc.vector.quantize_mx(codes[:, cols].bitcast(FP8X4), scales[:, cols], staging(key)[:, z * 512 : (z + 1) * 512])
+        def round_w2_direct(h, g):
+            nc.scalar.copy(
+                w2_direct[g][:, :, half_columns(h), :].rearrange("p t c j -> p c j t"), by_word(w2_in[h][g][:])[:, :, :, 2:4]
+            )
 
-        wide = {}
+        def round_half(dst, rows, h):
+            nc.scalar.copy(dst[:, :, half_columns(h), :].rearrange("p t c j -> p c j t"), by_word(rows))
 
-        def cast_all(m, z, h, eng):
-            if (m, z) not in wide:
-                stage[(m, z, 0)] = sb("wide%d_%d" % (m, z), [P, 2 * T], F32)
-                wide[(m, z)] = stage[(m, z, 0)][:].bitcast(BF16).rearrange("p (t c j) -> p t c j", t=PACK, j=PACK)
-                stage[(m, z, 1)] = stage[(m, z, 0)][:, T:]
-                stage[(m, z, 0)] = stage[(m, z, 0)][:, :T]
-            cast(wide[(m, z)][:, :, 64 * h : 64 * h + 64, :].rearrange("p t c j -> p c j t"), raw[(m, z, h)], eng)
+        def quantise_w1_turned(h, g):
+            for t in range(2):
+                values = w1_round[g][:, t, half_columns(h), :].rearrange("p c j -> p (c j)")
+                quantise(turned[1][h], g * P + t * HALF // PACK, values)
 
-        def operand(key):
-            if key not in wq:
-                name = "_".join(str(k) for k in key)
-                wq[key] = (sb("wc" + name, [P, 2 * P], U32), sb("ws" + name, [P, 2 * P], U8))
-            return wq[key]
+        def pair_of(rounded, u):
+            return rounded[:, 2 * u : 2 * u + 2].rearrange("p t c j -> p (t c j)")
 
-        def quant_a(m, h, z):
-            codes, scales = operand((m, "a", h))
-            for e in range(2):
-                cols = slice(z * P + 64 * e, z * P + 64 * e + 64)
-                nc.vector.quantize_mx(codes[:, cols].bitcast(FP8X4), scales[:, cols], wide[(m, z)][:, e, 64 * h : 64 * h + 64, :].rearrange("p c j -> p (c j)"))
-
-        def quant_b(m, z, pair=1):
-            codes, scales = operand((m, "b", z, pair))
-            nc.vector.quantize_mx(codes[:].bitcast(FP8X4), scales[:], wide[(m, z)][:, 2 * pair : 2 * pair + 2].rearrange("p t c j -> p (t c j)"))
-
-        def project(m, t, b):
-            acc = banks[b]
-            for z in range(PASSES):
-                codes, scales = wq[(m, "a", t)] if t < 2 else wq[(m, "b", z, 1)]
-                i = z if t < 2 else t - 2
-                cols = slice(i * P, (i + 1) * P)
+        def project(m, t, bank):
+            for g in range(PASSES):
+                codes, scales = turned[m][t] if t < 2 else direct[m][g]
+                first = (g if t < 2 else t - 2) * P
+                cols = slice(first, first + P)
                 nc.tensor.matmul_mx(
-                    acc[:], lhsT=codes[:, cols].bitcast(FP8X4), lhsT_scale=scales[:, cols],
-                    rhs=xw[:, z, :].bitcast(FP4X4), rhs_scale=xs[:, z, :], start=z == 0, stop=z == PASSES - 1,
+                    banks[bank][:], lhsT=codes[:, cols].bitcast(FP8X4), lhsT_scale=scales[:, cols],
+                    rhs=xw[:, g, :].bitcast(FP4X4), rhs_scale=xs[:, g, :], start=g == 0, stop=g == PASSES - 1,
                 )
-            nc.scalar.copy(e_win[t][:, :T] if m == 0 else y_sb[t][:], acc[:])
+            nc.scalar.copy(e_sb[t][:, :T] if m == 0 else y_sb[t][:], banks[bank][:])
 
-        early = {}
+        def neighbours(t, d, first, count):
+            return e_sb[t][:].indirect(lists[d][:, first // 16 : (first + count) // 16])
 
-        def window(t, d, v0, n):
-            return e_win[t][:].indirect(lists[d][:, v0 // 16 : (v0 + n) // 16])
+        fetched = {}
 
-        def fetch(h, d, held=None):
-            early[(h, d)] = sb("g%d_%d" % (h, d), [P, T], F32) if held is None else rawt[held[1:]] if held[0] == "raw" else stage[held]
-            nc.vector.tensor_copy(early[(h, d)][:], window(h, d, 0, T))
+        def fetch(h, d, room):
+            fetched[(h, d)] = room
+            nc.vector.tensor_copy(room, neighbours(h, d, 0, T))
 
-        act = [sb("act%d" % vb, [P, D, 2, 2 * P], BF16) for vb in range(VB)]
-        best = [sb("best%d" % vb, [P, 3, P], F32) for vb in range(VB)]
-        zb = [sb("zb%d" % vb, [P, P, 2], F32) for vb in range(VB)]
-        ub = {}
-        part = {}
-        obs = {}
+        for g in range(PASSES):
+            round_w2_turned(0, g, nc.vector.tensor_copy)
+            quantise(turned[0][0], g * P, w2_turned[0][:, g].rearrange("p t c j -> p (t c j)"))
+            round_w2_direct(0, g)
+        project(0, 0, 0)
+        round_w2_turned(1, 0, nc.vector.tensor_copy)
+        fetch(0, 0, sb("fetch00", [P, T], F32)[:])
+        round_w2_turned(1, 1, nc.scalar.copy)
+        both_passes = w2_turned[1][:].rearrange("p g t c j -> p (g t c j)")
+        quantise(turned[0][1], 0, both_passes)
+        fetch(0, 1, as_sums(both_passes))
+        for g in range(PASSES):
+            round_w2_direct(1, g)
+        fetch(0, 2, w2_in[1][1][:].rearrange("p j c -> p (j c)")[:, :T])
+        quantise(direct[0][1], 0, pair_of(w2_direct[1], 0))
+        fetch(0, 3, as_sums(pair_of(w2_direct[1], 0)))
+        quantise(direct[0][0], 0, pair_of(w2_direct[0], 0))
+        round_half(w1_round[0], w1_first[0][:], 0)
+        project(0, 1, 1)
+        round_half(w1_round[0], w1_first[1][:], 1)
+        project(0, 2, 7)
+        fetch(1, 0, as_sums(pair_of(w2_direct[0], 0)))
+        for h in range(2):
+            quantise_w1_turned(h, 0)
+        quantise(direct[1][0], 0, pair_of(w1_round[0], 1))
+        fetch(1, 1, as_sums(pair_of(w1_round[0], 0)))
+        for h in range(2):
+            round_half(w1_round[1], w1_second[:, :, h * HALF : (h + 1) * HALF], h)
+        quantise_w1_turned(0, 1)
+        quantise(direct[1][1], 0, pair_of(w1_round[1], 1))
+        quantise_w1_turned(1, 1)
+        for d in (2, 3):
+            fetch(1, d, w1_second[:, d - 2, :])
+        project(1, 0, 0)
+        project(1, 2, 2)
+        project(0, 3, 0)
+        project(1, 3, 3)
+        project(1, 1, 6)
 
-        def edge_a(h, vb, b):
-            bank = banks[b][:].rearrange("v (d c) -> v d c", d=D)
-            cols = slice(vb * P, (vb + 1) * P)
-            steps = [(d, y_sb[h][:, cols]) for d in range(D)] + [(d, early[(h, d)][:, cols]) for d in range(D)]
-            for i, (d, src) in enumerate(steps):
-                nc.tensor.matmul(bank[:, d, :], lhsT=src, rhs=ident[:], start=i == 0, stop=i == len(steps) - 1, is_transpose=True)
-            nc.scalar.activation(act[vb][:, :, 1, h * P : (h + 1) * P].rearrange("v d (c e) -> v d c e", e=2), bank.rearrange("v d (e c) -> v d c e", e=2), SILU)
-
-        def pool(vb, r0=0):
-            m = sb("m%d" % vb, [P, 2, 2 - r0, 2 * P], BF16)
-            nc.vector.tensor_tensor(m[:], act[vb][:, 0:2, r0:, :], act[vb][:, 2:4, r0:, :], MAX)
-            nc.vector.tensor_tensor(best[vb][:, 1 + r0 :, :].bitcast(BF16), m[:, 0], m[:, 1], MAX)
-
-        def back_a(vb, b):
-            nc.tensor.transpose(banks[b][:, :P], best[vb][:, 2, :], ident[:])
-            nc.scalar.copy(best[vb][:, 0, :], banks[b][:, :P])
-
-        def piece(vb, ds=range(D)):
-            for d in ds:
-                old = vb - 2 + d // 2
-                if old < 0:
-                    ub[(vb, d)] = sb("ub%d_%d" % (vb, d), [P, 2, P], F32)[:]
-                else:
-                    ub[(vb, d)] = act[old][:, d].rearrange("p r n -> p (r n)").bitcast(F32).rearrange("p (t v) -> p t v", t=2)
-                for t in (2, 3):
-                    nc.vector.tensor_tensor(ub[(vb, d)][:, t - 2, :], window(t, d, vb * P, P), y_sb[t][:, vb * P : (vb + 1) * P], ADD)
-                nc.scalar.activation(act[vb][:, d, 0, :].rearrange("p (v t) -> p v t", t=2), ub[(vb, d)].rearrange("p t v -> p v t"), SILU)
-
-        def pool_step(vb, d):
-            dst = sb("mp%d_%d" % (vb, d), [P, 2 * P], BF16)[:] if d < D - 1 else best[vb][:, 1, :].bitcast(BF16)
-            nc.vector.tensor_tensor(dst, act[vb][:, 0, 0, :] if d == 1 else part[vb], act[vb][:, d, 0, :], MAX)
-            part[vb] = dst
-
-        def weave(vb, eng="s"):
-            src = best[vb][:, 0:2, :].rearrange("p h v -> p v h")
-            if eng == "s":
-                nc.scalar.copy(zb[vb][:], src)
-            else:
-                nc.vector.tensor_copy(zb[vb][:], src)
-
-        oc = sb("oc", [P, T], U32)
-        os_ = sb("os", [P, T], U8)
+        act = [sb("act%d" % b, [P, D, 2, 2 * P], BF16) for b in range(BLOCKS)]
+        best = [sb("best%d" % b, [P, 3, P], F32) for b in range(BLOCKS)]
+        z_words = [sb("z%d" % b, [P, P, 2], F32) for b in range(BLOCKS)]
+        out_round = [sb("out_round%d" % b, [P, P, PACK], BF16) for b in range(BLOCKS)]
+        out_mx = mx_tiles("out_mx", T)
         out_rows = out_0.rearrange("(p t) v -> p t v", t=PACK)
         out_words = out_1[0].rearrange("p c r -> p (c r)").bitcast(I32)
 
-        def result(vb, how, b):
-            cols = slice(vb * P, (vb + 1) * P)
-            zc = sb("zc%d" % vb, [P, P], U32)
-            zs = sb("zs%d" % vb, [P, P], U8)
-            nc.vector.quantize_mx(zc[:].bitcast(FP8X4), zs[:], zb[vb][:].rearrange("p v h -> p (v h)").bitcast(BF16))
-            acc = banks[b][:].rearrange("p (t v) -> p t v", t=PACK)
+        def centres(b):
+            return slice(b * P, (b + 1) * P)
+
+        def turned_edges(h, b):
+            bank = banks[4 + h][:].rearrange("v (d c) -> v d c", d=D)
+            terms = [(d, y_sb[h][:, centres(b)]) for d in range(D)] + [(d, fetched[(h, d)][:, centres(b)]) for d in range(D)]
+            for n, (d, term) in enumerate(terms):
+                nc.tensor.matmul(bank[:, d, :], lhsT=term, rhs=ident[:], start=n == 0, stop=n == len(terms) - 1, is_transpose=True)
+            nc.scalar.activation(
+                act[b][:, :, 1, h * P : (h + 1) * P].rearrange("v d (c t) -> v d c t", t=2),
+                bank.rearrange("v d (t c) -> v d c t", t=2),
+                SILU,
+            )
+
+        def direct_edges(b, edges):
+            for d in edges:
+                old = b - 2 + d // 2
+                if old < 0:
+                    sums = sb("sums%d%d" % (b, d), [P, 2, P], F32)[:]
+                else:
+                    sums = act[old][:, d].rearrange("p r n -> p (r n)").bitcast(F32).rearrange("p (t v) -> p t v", t=2)
+                for t in (2, 3):
+                    nc.vector.tensor_tensor(sums[:, t - 2, :], neighbours(t, d, b * P, P), y_sb[t][:, centres(b)], ADD)
+                nc.scalar.activation(act[b][:, d, 0, :].rearrange("p (v t) -> p v t", t=2), sums.rearrange("p t v -> p v t"), SILU)
+
+        def largest(b, first_road):
+            two = sb("two%d" % b, [P, 2, 2 - first_road, 2 * P], BF16)
+            nc.vector.tensor_tensor(two[:], act[b][:, 0:2, first_road:, :], act[b][:, 2:4, first_road:, :], MAX)
+            nc.vector.tensor_tensor(best[b][:, 1 + first_road :, :].bitcast(BF16), two[:, 0], two[:, 1], MAX)
+
+        def turn_back(b, bank):
+            nc.tensor.transpose(banks[bank][:, :P], best[b][:, 2, :], ident[:])
+            nc.scalar.copy(best[b][:, 0, :], banks[bank][:, :P])
+
+        def weave(b, copy):
+            copy(z_words[b][:], best[b][:, 0:2, :].rearrange("p u v -> p v u"))
+
+        def multiply(b, slices):
+            z_mx = mx_tiles("z_mx%d" % b, P)
+            quantise(z_mx, 0, z_words[b][:].rearrange("p v u -> p (v u)").bitcast(BF16))
             for t in range(PACK):
-                codes, scales = wq[(2, "b", 0, t // 2)]
-                tc_ = slice((t % 2) * P, (t % 2 + 1) * P)
+                codes, scales = w3_mx[t // 2]
+                cols = slice((t % 2) * P, (t % 2 + 1) * P)
                 nc.tensor.matmul_mx(
-                    acc[:, t, :], lhsT=codes[:, tc_].bitcast(FP8X4), lhsT_scale=scales[:, tc_],
-                    rhs=zc[:].bitcast(FP8X4), rhs_scale=zs[:], start=True, stop=True,
+                    slices[t], lhsT=codes[:, cols].bitcast(FP8X4), lhsT_scale=scales[:, cols],
+                    rhs=z_mx[0][:].bitcast(FP8X4), rhs_scale=z_mx[1][:], start=True, stop=True,
                 )
-            o32 = sb("o32_%d" % vb, [P, PACK, P], F32)
-            ob = sb("ob%d" % vb, [P, P, PACK], BF16)
-            if how == "p":
-                nc.vector.tensor_copy(ob[:], acc.rearrange("p t v -> p v t"))
-            elif how == "s":
-                nc.scalar.copy(ob[:], acc.rearrange("p t v -> p v t"))
-            nc.scalar.copy(o32[:], acc)
-            nc.sync.dma_start(out_rows[:, :, cols], o32[:])
-            if how in "vg":
-                cast(ob[:].rearrange("p (c i) t -> p c t i", i=4), o32[:].rearrange("p t (c i) -> p c t i", i=4), how)
-            obs[vb] = ob
 
-        def last_result(vb, b0, b1):
-            cols = slice(vb * P, (vb + 1) * P)
-            zc = sb("zc%d" % vb, [P, P], U32)
-            zs = sb("zs%d" % vb, [P, P], U8)
-            nc.vector.quantize_mx(zc[:].bitcast(FP8X4), zs[:], zb[vb][:].rearrange("p v h -> p (v h)").bitcast(BF16))
-            accs = [banks[b][:, : 2 * P].rearrange("p (t v) -> p t v", t=2) for b in (b0, b1)]
-            for t in range(PACK):
-                codes, scales = wq[(2, "b", 0, t // 2)]
-                tc_ = slice((t % 2) * P, (t % 2 + 1) * P)
-                nc.tensor.matmul_mx(
-                    accs[t // 2][:, t % 2, :], lhsT=codes[:, tc_].bitcast(FP8X4), lhsT_scale=scales[:, tc_],
-                    rhs=zc[:].bitcast(FP8X4), rhs_scale=zs[:], start=True, stop=True,
-                )
-            o32 = sb("o32_%d" % vb, [P, PACK, P], F32)
-            ob = sb("ob%d" % vb, [P, P, PACK], BF16)
-            nc.scalar.copy(o32[:, 0:2, :], accs[0])
-            nc.vector.tensor_copy(o32[:, 2:4, :], accs[1])
-            nc.scalar.dma_start(out_rows[:, :, cols], o32[:])
-            cast(ob[:].rearrange("p (c i) t -> p c t i", i=4), o32[:].rearrange("p t (c i) -> p c t i", i=4), "v")
-            obs[vb] = ob
+        def result(b):
+            bank = banks[6 + b % 2][:].rearrange("p (t v) -> p t v", t=PACK)
+            multiply(b, [bank[:, t, :] for t in range(PACK)])
+            values = sb("values%d" % b, [P, PACK, P], F32)
+            nc.scalar.copy(out_round[b][:], bank.rearrange("p t v -> p v t"))
+            nc.scalar.copy(values[:], bank)
+            nc.sync.dma_start(out_rows[:, :, centres(b)], values[:])
 
-        def planes(vb):
-            cols = slice(vb * P, (vb + 1) * P)
-            nc.vector.quantize_mx(oc[:, cols].bitcast(FP8X4), os_[:, cols], obs[vb][:].rearrange("p v t -> p (v t)"))
-            nc.sync.dma_start(out_words[:, cols], oc[:, cols].bitcast(I32))
+        def planes(b):
+            quantise(out_mx, b * P, out_round[b][:].rearrange("p v t -> p (v t)"))
+            nc.sync.dma_start(out_words[:, centres(b)], out_mx[0][:, centres(b)].bitcast(I32))
 
-        cast_a(0, 0, 0, "v")
-        quant((0, "a", 0), 0)
-        cast_b(0, 0, "s", 0)
-        cast_a(0, 0, 1, "v")
-        quant((0, "a", 0), 1)
-        cast_b(0, 1, "s", 0)
-        project(0, 0, 0)
-        cast_a(0, 1, 0, "v")
-        fetch(0, 0)
-        cast_a(0, 1, 1, "s")
-        quant((0, "a", 1))
-        fetch(0, 1, (0, "a", 1))
-        cast_b(0, 0, "s", 1)
-        cast_b(0, 1, "s", 1)
-        project(0, 1, 1)
-        fetch(0, 2, ("raw", 0, 1, 1))
-        quant((0, "b", 1, 1))
-        fetch(0, 3, (0, "b", 1, 1))
-        quant((0, "b", 0, 1))
-        cast_all(1, 0, 0, "s")
-        cast_all(1, 0, 1, "s")
-        fetch(1, 0, (0, "b", 0, 1))
-        cast_all(1, 1, 0, "s")
-        quant_a(1, 0, 0)
-        quant_a(1, 1, 0)
-        quant_b(1, 0)
-        quant_a(1, 0, 1)
-        fetch(1, 1, (1, 0, 0))
-        cast_all(1, 1, 1, "s")
-        project(1, 0, 0)
-        quant_a(1, 1, 1)
-        quant_b(1, 1)
-        fetch(1, 2, (1, 1, 1))
-        fetch(1, 3, (1, 1, 0))
-        project(0, 2, 0)
-        project(1, 2, 2)
-        project(0, 3, 1)
-        project(1, 3, 3)
-        project(1, 1, 6)
-        edge_a(0, 0, 4)
-        cast_all(2, 0, 0, "s")
-        edge_a(1, 0, 5)
-        piece(0)
-        edge_a(0, 1, 4)
-        piece(1, range(2))
-        pool(0)
-        back_a(0, 1)
-        edge_a(1, 1, 5)
-        cast_all(2, 0, 1, "s")
-        quant_b(2, 0, 0)
-        quant_b(2, 0, 1)
-        weave(0)
-        piece(1, range(2, 4))
-        edge_a(0, 2, 4)
-        piece(2, range(2))
-        pool(1)
-        result(0, "s", 6)
-        back_a(1, 1)
-        edge_a(1, 2, 5)
-        weave(1)
-        piece(2, range(2, 4))
-        planes(0)
-        edge_a(0, 3, 4)
-        edge_a(1, 3, 5)
-        piece(3, range(2))
-        pool(2)
-        result(1, "s", 7)
-        back_a(2, 1)
-        pool(3, 1)
-        weave(2)
-        pool_step(3, 1)
-        piece(3, range(2, 3))
-        planes(1)
-        result(2, "s", 6)
-        piece(3, range(3, 4))
-        back_a(3, 2)
-        pool_step(3, 2)
-        pool_step(3, 3)
-        weave(3, "v")
-        planes(2)
-        last_result(3, 7, 0)
-        planes(3)
+        last = BLOCKS - 1
+        turned_edges(0, 0)
+        round_half(w3_round, w3_in[:, :, :HALF], 0)
+        turned_edges(1, 0)
+        direct_edges(0, range(D))
+        for b in range(last - 1):
+            turned_edges(0, b + 1)
+            direct_edges(b + 1, (0, 1))
+            largest(b, 0)
+            if b > 0:
+                result(b - 1)
+            turn_back(b, 1)
+            turned_edges(1, b + 1)
+            if b == 0:
+                round_half(w3_round, w3_in[:, :, HALF:], 1)
+                for u in range(2):
+                    quantise(w3_mx[u], 0, pair_of(w3_round, u))
+            weave(b, nc.scalar.copy)
+            direct_edges(b + 1, (2, 3))
+            if b > 0:
+                planes(b - 1)
+
+        for h in range(2):
+            turned_edges(h, last)
+        direct_edges(last, (0, 1))
+        largest(last - 1, 0)
+        result(last - 2)
+        turn_back(last - 1, 1)
+        largest(last, 1)
+        weave(last - 1, nc.scalar.copy)
+        so_far = [sb("so_far%d" % n, [P, 2 * P], BF16) for n in range(2)]
+        nc.vector.tensor_tensor(so_far[0][:], act[last][:, 0, 0, :], act[last][:, 1, 0, :], MAX)
+        direct_edges(last, (2,))
+        planes(last - 2)
+        result(last - 1)
+        direct_edges(last, (3,))
+        turn_back(last, 2)
+        nc.vector.tensor_tensor(so_far[1][:], so_far[0][:], act[last][:, 2, 0, :], MAX)
+        nc.vector.tensor_tensor(best[last][:, 1, :].bitcast(BF16), so_far[1][:], act[last][:, 3, 0, :], MAX)
+        weave(last, nc.vector.tensor_copy)
+        planes(last - 1)
+        halves = [banks[bank][:, : 2 * P].rearrange("p (t v) -> p t v", t=2) for bank in (7, 0)]
+        multiply(last, [halves[t // 2][:, t % 2, :] for t in range(PACK)])
+        values = sb("values_last", [P, PACK, P], F32)
+        nc.scalar.copy(values[:, 0:2, :], halves[0])
+        nc.vector.tensor_copy(values[:, 2:4, :], halves[1])
+        nc.scalar.dma_start(out_rows[:, :, centres(last)], values[:])
+        nc.vector.tensor_copy(
+            out_round[last][:].rearrange("p (c i) t -> p c t i", i=4), values[:].rearrange("p t (c i) -> p c t i", i=4)
+        )
+        planes(last)
+
         for q in range(4):
-            eng = nc.sync if q % 2 == 0 else nc.scalar
-            eng.dma_start(out_2[0, 4 * q : 4 * q + 4, :].bitcast(I32), os_[32 * q : 32 * q + 4, :].bitcast(I32))
+            queue = nc.sync if q % 2 == 0 else nc.scalar
+            queue.dma_start(out_2[0, 4 * q : 4 * q + 4, :].bitcast(I32), out_mx[1][32 * q : 32 * q + 4, :].bitcast(I32))

from contextlib import ExitStack

import concourse.mybir as mybir
from concourse.masks import make_identity

K, T, H, D = 1024, 512, 512, 4
P = 128
PACK = 4
PASSES = K // (P * PACK)
BLOCKS = T // P
HALF = H // 2
WIDE = 704

FLOPS = 2 * K * H * T * 2 + 2 * H * H * T

F32 = mybir.dt.float32
BF16 = mybir.dt.bfloat16
I32 = mybir.dt.int32
U32 = mybir.dt.uint32
U16 = mybir.dt.uint16
U8 = mybir.dt.uint8
FP8X4 = mybir.dt.float8_e4m3fn_x4
FP4X4 = mybir.dt.float4_e2m1fn_x4
SILU = mybir.ActivationFunctionType.Silu
MAX = mybir.AluOpType.max
ADD = mybir.AluOpType.add


def tile_picked_wedgecv_silu_lo_kernel(
    tc, x_words, x_scales, w1, w2, w3, pos1, pos2, pos3, pos4, out_0, out_1, out_2
):
    nc = tc.nc
    with ExitStack() as ctx:
        keep = ctx.enter_context(tc.tile_pool(name="keep", bufs=1))
        psum = ctx.enter_context(tc.psum_pool(name="psum", bufs=1))

        def sb(name, shape, dtype, tag=None):
            return keep.tile(shape, dtype, name=name, tag=tag or name, align_bytes=64)

        def mx_tiles(name, columns):
            return sb(name + "_codes", [P, columns], U32), sb(name + "_scales", [P, columns], U8)

        def quantise(operand, first, values):
            cols = slice(first, first + values.shape[1] // PACK)
            nc.vector.quantize_mx(operand[0][:, cols].bitcast(FP8X4), operand[1][:, cols], values)

        def as_sums(view):
            return view.bitcast(F32)[:, :T]

        lists = [sb("list%d" % d, [P, T // 16], U16) for d in range(D)]
        xw = sb("xw", [P, PASSES, 2 * T], U8)
        xs = sb("xs", [P, PASSES, T], U8)
        ident = sb("ident", [P, P], F32)
        zeros = sb("zeros", [P, WIDE - T], F32)
        e_sb = [sb("e%d" % h, [P, WIDE], F32) for h in range(2)]
        y_sb = [sb("y%d" % t, [P, T], F32) for t in range(PACK)]
        banks = [psum.tile([P, T], F32, name="bank%d" % b) for b in range(8)]

        nc.gpsimd.memset(xs[:].bitcast(I32), 0)
        for q in range(4):
            nc.scalar.dma_start(
                xs[32 * q : 32 * q + 4, :, :].bitcast(I32),
                x_scales[:, 4 * q : 4 * q + 4, :].rearrange("g r c -> r g c").bitcast(I32),
            )
        nc.gpsimd.memset(zeros[:], 0.0)
        make_identity(nc, ident[:])
        for h in range(2):
            nc.scalar.activation(e_sb[h][:, T:], zeros[:], SILU)

        def load_rows(name, w, g, first, columns):
            rows = sb(name, [P, PACK, columns], F32)
            nc.sync.dma_start(
                rows[:], w[g * P * PACK : (g + 1) * P * PACK, first : first + columns].rearrange("(p j) c -> p j c", j=PACK)
            )
            return rows

        def load_list(d):
            nc.sync.dma_start(lists[d][:], (pos1, pos2, pos3, pos4)[d])

        w2_in = [[load_rows("w2_0%d" % g, w2, g, 0, HALF) for g in range(PASSES)]]
        nc.sync.dma_start(xw[:].bitcast(I32), x_words.rearrange("g p b -> p g b").bitcast(I32))
        load_list(0)
        w2_in.append([load_rows("w2_10", w2, 0, HALF, HALF)])
        load_list(1)
        w2_in[1].append(load_rows("w2_11", w2, 1, HALF, HALF))
        w1_first = [load_rows("w1_00", w1, 0, 0, HALF)]
        load_list(2)
        w1_first.append(load_rows("w1_01", w1, 0, HALF, HALF))
        load_list(3)
        w1_second = load_rows("w1_1", w1, 1, 0, H)
        w3_in = load_rows("w3_in", w3, 0, 0, H)

        e_sb.append(sb("e2", [P, T], F32, "w1_01"))
        e_sb.append(sb("e3", [P, T], F32))

        def by_word(rows):
            return rows.rearrange("p j (c t) -> p c j t", t=PACK)

        w2_turned = [sb("w2_turned%d" % h, [P, PASSES, 2, HALF // PACK, PACK], BF16) for h in range(2)]
        w2_direct = [sb("w2_direct%d" % g, [P, 2, P, PACK], BF16) for g in range(PASSES)]
        w1_round = [sb("w1_round%d" % g, [P, PACK, P, PACK], BF16) for g in range(PASSES)]
        w3_round = sb("w3_round", [P, PACK, P, PACK], BF16)
        turned = [[mx_tiles("turned%d%d" % (m, h), PASSES * P) for h in range(2)] for m in range(2)]
        direct = [[mx_tiles("direct%d%d" % (m, g), 2 * P) for g in range(PASSES)] for m in range(2)]
        w3_mx = [mx_tiles("w3_mx%d" % u, 2 * P) for u in range(2)]

        def half_columns(h):
            return slice(h * HALF // PACK, (h + 1) * HALF // PACK)

        def round_w2_turned(h, g, copy):
            copy(w2_turned[h][:, g].rearrange("p t c j -> p c j t"), by_word(w2_in[h][g][:])[:, :, :, 0:2])

        def round_w2_direct(h, g):
            nc.scalar.copy(
                w2_direct[g][:, :, half_columns(h), :].rearrange("p t c j -> p c j t"), by_word(w2_in[h][g][:])[:, :, :, 2:4]
            )

        def round_half(dst, rows, h):
            nc.scalar.copy(dst[:, :, half_columns(h), :].rearrange("p t c j -> p c j t"), by_word(rows))

        def quantise_w1_turned(h, g):
            for t in range(2):
                values = w1_round[g][:, t, half_columns(h), :].rearrange("p c j -> p (c j)")
                quantise(turned[1][h], g * P + t * HALF // PACK, values)

        def pair_of(rounded, u):
            return rounded[:, 2 * u : 2 * u + 2].rearrange("p t c j -> p (t c j)")

        def project(m, t, bank):
            for g in range(PASSES):
                codes, scales = turned[m][t] if t < 2 else direct[m][g]
                first = (g if t < 2 else t - 2) * P
                cols = slice(first, first + P)
                nc.tensor.matmul_mx(
                    banks[bank][:], lhsT=codes[:, cols].bitcast(FP8X4), lhsT_scale=scales[:, cols],
                    rhs=xw[:, g, :].bitcast(FP4X4), rhs_scale=xs[:, g, :], start=g == 0, stop=g == PASSES - 1,
                )
            nc.scalar.copy(e_sb[t][:, :T] if m == 0 else y_sb[t][:], banks[bank][:])

        def neighbours(t, d, first, count):
            return e_sb[t][:].indirect(lists[d][:, first // 16 : (first + count) // 16])

        fetched = {}

        def fetch(h, d, room):
            fetched[(h, d)] = room
            nc.vector.tensor_copy(room, neighbours(h, d, 0, T))

        for g in range(PASSES):
            round_w2_turned(0, g, nc.vector.tensor_copy)
            quantise(turned[0][0], g * P, w2_turned[0][:, g].rearrange("p t c j -> p (t c j)"))
            round_w2_direct(0, g)
        project(0, 0, 0)
        round_w2_turned(1, 0, nc.vector.tensor_copy)
        fetch(0, 0, sb("fetch00", [P, T], F32)[:])
        round_w2_turned(1, 1, nc.scalar.copy)
        both_passes = w2_turned[1][:].rearrange("p g t c j -> p (g t c j)")
        quantise(turned[0][1], 0, both_passes)
        fetch(0, 1, as_sums(both_passes))
        for g in range(PASSES):
            round_w2_direct(1, g)
        fetch(0, 2, w2_in[1][1][:].rearrange("p j c -> p (j c)")[:, :T])
        quantise(direct[0][1], 0, pair_of(w2_direct[1], 0))
        fetch(0, 3, as_sums(pair_of(w2_direct[1], 0)))
        quantise(direct[0][0], 0, pair_of(w2_direct[0], 0))
        round_half(w1_round[0], w1_first[0][:], 0)
        project(0, 1, 1)
        round_half(w1_round[0], w1_first[1][:], 1)
        project(0, 2, 7)
        fetch(1, 0, as_sums(pair_of(w2_direct[0], 0)))
        for h in range(2):
            quantise_w1_turned(h, 0)
        quantise(direct[1][0], 0, pair_of(w1_round[0], 1))
        fetch(1, 1, as_sums(pair_of(w1_round[0], 0)))
        for h in range(2):
            round_half(w1_round[1], w1_second[:, :, h * HALF : (h + 1) * HALF], h)
        quantise_w1_turned(0, 1)
        quantise(direct[1][1], 0, pair_of(w1_round[1], 1))
        quantise_w1_turned(1, 1)
        for d in (2, 3):
            fetch(1, d, w1_second[:, d - 2, :])
        project(1, 0, 0)
        project(1, 2, 2)
        project(0, 3, 0)
        project(1, 3, 3)
        project(1, 1, 6)

        act = [sb("act%d" % b, [P, D, 2, 2 * P], BF16) for b in range(BLOCKS)]
        best = [sb("best%d" % b, [P, 3, P], F32) for b in range(BLOCKS)]
        z_words = [sb("z%d" % b, [P, P, 2], F32) for b in range(BLOCKS)]
        out_round = [sb("out_round%d" % b, [P, P, PACK], BF16) for b in range(BLOCKS)]
        out_mx = mx_tiles("out_mx", T)
        out_rows = out_0.rearrange("(p t) v -> p t v", t=PACK)
        out_words = out_1[0].rearrange("p c r -> p (c r)").bitcast(I32)

        def centres(b):
            return slice(b * P, (b + 1) * P)

        def turned_edges(h, b):
            bank = banks[4 + h][:].rearrange("v (d c) -> v d c", d=D)
            terms = [(d, y_sb[h][:, centres(b)]) for d in range(D)] + [(d, fetched[(h, d)][:, centres(b)]) for d in range(D)]
            for n, (d, term) in enumerate(terms):
                nc.tensor.matmul(bank[:, d, :], lhsT=term, rhs=ident[:], start=n == 0, stop=n == len(terms) - 1, is_transpose=True)
            nc.scalar.activation(
                act[b][:, :, 1, h * P : (h + 1) * P].rearrange("v d (c t) -> v d c t", t=2),
                bank.rearrange("v d (t c) -> v d c t", t=2),
                SILU,
            )

        def direct_edges(b, edges):
            for d in edges:
                old = b - 2 + d // 2
                if old < 0:
                    sums = sb("sums%d%d" % (b, d), [P, 2, P], F32)[:]
                else:
                    sums = act[old][:, d].rearrange("p r n -> p (r n)").bitcast(F32).rearrange("p (t v) -> p t v", t=2)
                for t in (2, 3):
                    nc.vector.tensor_tensor(sums[:, t - 2, :], neighbours(t, d, b * P, P), y_sb[t][:, centres(b)], ADD)
                nc.scalar.activation(act[b][:, d, 0, :].rearrange("p (v t) -> p v t", t=2), sums.rearrange("p t v -> p v t"), SILU)

        def largest(b, first_road):
            two = sb("two%d" % b, [P, 2, 2 - first_road, 2 * P], BF16)
            nc.vector.tensor_tensor(two[:], act[b][:, 0:2, first_road:, :], act[b][:, 2:4, first_road:, :], MAX)
            nc.vector.tensor_tensor(best[b][:, 1 + first_road :, :].bitcast(BF16), two[:, 0], two[:, 1], MAX)

        def turn_back(b, bank):
            nc.tensor.transpose(banks[bank][:, :P], best[b][:, 2, :], ident[:])
            nc.scalar.copy(best[b][:, 0, :], banks[bank][:, :P])

        def weave(b, copy):
            copy(z_words[b][:], best[b][:, 0:2, :].rearrange("p u v -> p v u"))

        def multiply(b, slices):
            z_mx = mx_tiles("z_mx%d" % b, P)
            quantise(z_mx, 0, z_words[b][:].rearrange("p v u -> p (v u)").bitcast(BF16))
            for t in range(PACK):
                codes, scales = w3_mx[t // 2]
                cols = slice((t % 2) * P, (t % 2 + 1) * P)
                nc.tensor.matmul_mx(
                    slices[t], lhsT=codes[:, cols].bitcast(FP8X4), lhsT_scale=scales[:, cols],
                    rhs=z_mx[0][:].bitcast(FP8X4), rhs_scale=z_mx[1][:], start=True, stop=True,
                )

        def result(b):
            bank = banks[6 + b % 2][:].rearrange("p (t v) -> p t v", t=PACK)
            multiply(b, [bank[:, t, :] for t in range(PACK)])
            values = sb("values%d" % b, [P, PACK, P], F32)
            nc.scalar.copy(out_round[b][:], bank.rearrange("p t v -> p v t"))
            nc.scalar.copy(values[:], bank)
            nc.sync.dma_start(out_rows[:, :, centres(b)], values[:])

        def planes(b):
            quantise(out_mx, b * P, out_round[b][:].rearrange("p v t -> p (v t)"))
            nc.sync.dma_start(out_words[:, centres(b)], out_mx[0][:, centres(b)].bitcast(I32))

        last = BLOCKS - 1
        turned_edges(0, 0)
        round_half(w3_round, w3_in[:, :, :HALF], 0)
        turned_edges(1, 0)
        direct_edges(0, range(D))
        for b in range(last - 1):
            turned_edges(0, b + 1)
            direct_edges(b + 1, (0, 1))
            largest(b, 0)
            if b > 0:
                result(b - 1)
            turn_back(b, 1)
            turned_edges(1, b + 1)
            if b == 0:
                round_half(w3_round, w3_in[:, :, HALF:], 1)
                for u in range(2):
                    quantise(w3_mx[u], 0, pair_of(w3_round, u))
            weave(b, nc.scalar.copy)
            direct_edges(b + 1, (2, 3))
            if b > 0:
                planes(b - 1)

        for h in range(2):
            turned_edges(h, last)
        direct_edges(last, (0, 1))
        largest(last - 1, 0)
        result(last - 2)
        turn_back(last - 1, 1)
        largest(last, 1)
        weave(last - 1, nc.scalar.copy)
        so_far = [sb("so_far%d" % n, [P, 2 * P], BF16) for n in range(2)]
        nc.vector.tensor_tensor(so_far[0][:], act[last][:, 0, 0, :], act[last][:, 1, 0, :], MAX)
        direct_edges(last, (2,))
        planes(last - 2)
        result(last - 1)
        direct_edges(last, (3,))
        turn_back(last, 2)
        nc.vector.tensor_tensor(so_far[1][:], so_far[0][:], act[last][:, 2, 0, :], MAX)
        nc.vector.tensor_tensor(best[last][:, 1, :].bitcast(BF16), so_far[1][:], act[last][:, 3, 0, :], MAX)
        weave(last, nc.vector.tensor_copy)
        planes(last - 1)
        halves = [banks[bank][:, : 2 * P].rearrange("p (t v) -> p t v", t=2) for bank in (7, 0)]
        multiply(last, [halves[t // 2][:, t % 2, :] for t in range(PACK)])
        values = sb("values_last", [P, PACK, P], F32)
        nc.scalar.copy(values[:, 0:2, :], halves[0])
        nc.vector.tensor_copy(values[:, 2:4, :], halves[1])
        nc.scalar.dma_start(out_rows[:, :, centres(last)], values[:])
        nc.vector.tensor_copy(
            out_round[last][:].rearrange("p (c i) t -> p c t i", i=4), values[:].rearrange("p t (c i) -> p c t i", i=4)
        )
        planes(last)

        for q in range(4):
            queue = nc.sync if q % 2 == 0 else nc.scalar
            queue.dma_start(out_2[0, 4 * q : 4 * q + 4, :].bitcast(I32), out_mx[1][32 * q : 32 * q + 4, :].bitcast(I32))
